import numpy as np, ml_dtypes
CORES = [2,6,10,14,18,22,26,30]
N = 8
BF = ml_dtypes.bfloat16
M, L, S, E, G0, T, Q, W = 3264, 96, 32, 5, 3, 4, 1056, 3376
LV = [320, 640, 864, 864, 512]
def forest(rng, lean):
    sn = np.full((16, M), M); fa = rng.integers(0, M, M); gn = np.zeros(M, np.int64)
    o = 64 + rng.permutation(M - 64); cur = np.arange(64); at = 0
    for i, n in enumerate(LV):
        nxt = o[at:at + n]; at += n
        share = 0.9 if i == 0 else 0.45 + 0.3 * rng.random()
        fert = rng.permutation(cur)[:max(n // 16 + 1, int(len(cur) * share))]
        key = rng.random((len(fert), 16)) * np.exp2(lean * rng.random((len(fert), 1)))
        pk = np.argsort(key.reshape(-1))[:n]; dad = fert[pk >> 4]
        sn[pk & 15, dad] = nxt; fa[nxt] = dad; gn[nxt] = i + 1; cur = nxt
    return sn, fa, gn
def woods(rng, lean):
    v = [forest(rng, lean) for _ in range(8 * N)]
    return np.stack([a[0] for a in v]).reshape(N, 8, 16, M), np.stack([a[1] for a in v]).reshape(N, 8, M), np.stack([a[2] for a in v]).reshape(N, 8, M)
def pack(x, w, sn, fa, gn):
    return {"x": np.ascontiguousarray(x.reshape(N, 128, M)).astype(np.float32).astype(BF), "w": np.ascontiguousarray(w.reshape(N, 128, 1)).astype(np.float32).astype(BF),
            "sn": np.ascontiguousarray(sn.reshape(N, 128, M)).astype(np.int32), "fa": fa.astype(np.int32), "gn": gn.astype(np.int32)}
def few(rng, sn, fa, gn, n):
    if n: sn[:, 64] = M; sn[:, M - 1] = M
    z = int(rng.integers(0, 64)); sn[:, z] = M
    empty = np.all(sn == M, axis=0); gn[empty] = np.minimum(gn[empty], G0 - 1)
    if n:
        o = np.flatnonzero(empty); o = rng.permutation(o[(o > 64) & (o < M - 1)])[:n - 2]
        o = np.concatenate([np.array([64, M - 1]), o]); fa[o] = z; gn[o] = G0 + rng.integers(0, 2, len(o))
def ladders(rng, sn, fa, gn):
    U = (E - 2) // 2 + 1; B = 2 * U + 4; nb = (M - 64) // B
    sn[:] = M; gn[:] = 0; fa[:] = rng.integers(0, 64, M)
    k = (64 + rng.permutation(M - 64))[:nb * B].reshape(nb, B); u = rng.integers(0, U + 1, nb); a = rng.integers(0, 16, nb)
    for j in range(U + 1):
        m = j <= u; up = k[m, j]; so = k[m, 1 + j]
        sn[a[m] if j == 0 else rng.integers(0, 16, len(up)), up] = so; fa[so] = up
    a = (a + 1 + rng.integers(0, 15, nb)) & 15
    for j in range(U + 2):
        m = j <= u + 1; up = k[m, 0 if j == 0 else U + 1 + j]; so = k[m, U + 2 + j]
        sn[a[m] if j == 0 else rng.integers(0, 16, len(up)), up] = so; fa[so] = up
    gn[k[np.arange(nb), 1 + u]] = G0 + rng.integers(0, 2, nb)
    sn[:4, :64] = rng.choice(k[:, 0], (4, 64))
def guests(rng, x, sn, fa, gn):
    n = S - int(rng.integers(0, 4)); z = int(rng.integers(1, 64)); o = 64 + rng.permutation(M - 64)
    last = M - 16 - np.arange(n); o = np.concatenate([last, o[~np.isin(o, last)]])
    s, p, q, y, h, r, u, v = o[:8 * n].reshape(8, n); h = np.sort(h)
    x[:] = rng.integers(0, 256, (16, M)); sn[:] = M; fa[:] = rng.integers(0, M, M); gn[:] = rng.integers(0, G0, M)
    deck = [np.arange(64)] + np.array_split(o[8 * n:], E)
    for a, b in zip(deck[:-1], deck[1:]):
        m = rng.random((16, len(a))) < 0.3; m[rng.integers(0, 16, len(a)), np.arange(len(a))] = True
        sn[:, a] = np.where(m, rng.choice(b, (16, len(a))), M); fa[b] = rng.choice(a, len(b))
    sn[:, z] = M
    for top, one, two in ((p, q, y), (y, h, r), (r, s, u)):
        i = rng.integers(0, 16, n); j = (i + rng.integers(1, 16, n)) & 15
        sn[i, top] = one; sn[j, top] = two; fa[one] = top; fa[two] = top
    sn[rng.integers(0, 16, n), s] = v; fa[v] = s; fa[h] = z; gn[q] = G0; gn[h] = G0
    x[:, h] = x[:, q]; x[:, r] = 255 - x[:, q]; x[:, u] = 255 - x[:, q]
    x[:, s] = x[:, q]; x[:8, s] = x[:8, s] ^ rng.integers(0, 2, (8, n))
def doubles(rng, o, x, sn, fa, gn, nought):
    n = len(o) // 8; p, g, y, z, v, u, a, b = o[:8 * n].reshape(8, n)
    h = 1 + rng.permutation(31)[:n]
    if nought: h[0] = 0
    sn[:, o] = M; sn[:, h] = M; fa[h] = p; fa[p] = g; gn[h] = G0
    up = np.arange(n) % 2 == 1; top = np.where(up, g, p); low = np.where(up, p, h); k = np.argsort(rng.random((n, 16)), axis=1).T
    sn[k[0], top] = low; sn[k[1], top] = low; sn[np.minimum(k[2], k[3]), top] = z; sn[np.maximum(k[2], k[3]), top] = y
    sn[k[4][up], p[up]] = h[up]; sn[k[5][up], p[up]] = h[up]
    sn[k[6], y] = v; sn[k[7], z] = u; sn[k[8], v] = a; sn[k[9], u] = b
    end = 255 * rng.integers(0, 2, (16, n)); m = rng.integers(0, 64, (16, n)) * ((np.arange(n) // 2) % 2)
    one = np.zeros((16, n), np.int64); one[rng.integers(0, 16, n), np.arange(n)] = 1
    x[:, h] = end; x[:, p] = end; x[:, z] = np.abs(255 - end - m); x[:, y] = np.abs(255 - end - m - one)
    return h
def setup_inputs(rng):
    sn, fa, gn = woods(rng, 3.0)
    return pack(rng.integers(0, 256, (N, 8, 16, M)), rng.integers(0, 16, (N, 8, 16, 1)), sn, fa, gn)
def setup_inputs_again(rng):
    sn, fa, gn = woods(rng, 2.0); base = rng.choice(np.array([0, 7, 130, 254]), (N, 8, 1, 1))
    x = base + np.where(rng.random((N, 8, 1, M)) < 0.75, rng.integers(0, 2, (N, 8, 1, M)), rng.integers(0, 2, (N, 8, 16, M)))
    for g in rng.permutation(8)[:4]:
        for q in range(N): guests(rng, x[q, g], sn[q, g], fa[q, g], gn[q, g])
    return pack(x, rng.integers(0, 16, (N, 8, 16, 1)), sn, fa, gn)
def setup_inputs_corners(rng):
    sn, fa, gn = woods(rng, 3.0)
    for q in range(N):
        for g, kind in enumerate(rng.permutation(8)):
            s, f_, n_ = sn[q, g], fa[q, g], gn[q, g]
            if kind < 6: few(rng, s, f_, n_, (S, S + 1, S - 1, L, L + 1, 0)[int(kind)])
            elif kind == 6:
                half = rng.permutation(M)[:M // 2]; s[:] = M; s[:, half] = rng.integers(0, M, (16, len(half)))
                f_[:] = rng.choice(half, M); n_[:] = rng.integers(0, E + 1, M)
            else: ladders(rng, s, f_, n_)
    return pack(rng.integers(0, 256, (N, 8, 16, M)), rng.integers(0, 16, (N, 8, 16, 1)), sn, fa, gn)
def setup_inputs_ends(rng):
    w = 15 * rng.integers(0, 2, (N, 8, 16, 1))
    for q in range(N):
        full, none = rng.permutation(8)[:2]
        if q == N - 1: full, none = 7, 0
        w[q, full] = 15; w[q, none] = 0
    x = 255 * np.where(rng.random((N, 8, 1, M)) < 0.6, rng.integers(0, 2, (N, 8, 1, M)), rng.integers(0, 2, (N, 8, 16, M))); x[..., 0] = 0; x[..., M - 1] = 255
    gn = E * rng.integers(0, 2, (N, 8, M)); sn = np.full((N, 8, 16, M), M)
    fa = np.where(rng.random((N, 8, M)) < 0.68, (M - 1) * rng.integers(0, 2, (N, 8, M)), rng.integers(0, M, (N, 8, M)))
    for q in range(N):
        for g in range(8):
            fer = rng.random(M) < 0.45; fer[:64] = True; fer[M - 1] = g % 2 == 0; fc = np.flatnonzero(fer)
            u = rng.random(M); m = rng.random((16, M)) < 0.3; m[:, u < 0.25] = False; m[15, u < 0.25] = True; m[:, u > 0.9] = True
            v = np.where(rng.random((16, M)) < 0.75, rng.choice(fc, (16, M)), rng.integers(0, M, (16, M)))
            v = np.where(rng.random((16, M)) < 0.12, (M - 1) * rng.integers(0, 2, (16, M)), v)
            sn[q, g] = np.where(m & fer, v, M); sn[q, g, 15, 0] = 0
            if g % 2 == 0:
                far = fc[np.all(x[q, g][:, fc] == 255, axis=0)]; sn[q, g, :, M - 1] = rng.choice(far, 16)
            else: gn[q, g, M - 1] = E; fa[q, g, M - 1] = rng.choice(fc)
    return pack(x, w, sn, fa, gn)
def setup_inputs_loops(rng):
    fa = rng.integers(0, M, (N, 8, M)); fa = np.where(rng.random((N, 8, M)) < 0.05, np.arange(M), fa)
    gn = rng.integers(0, E + 1, (N, 8, M)); sn = np.full((N, 8, 16, M), M); x = rng.integers(0, 256, (N, 8, 16, M))
    for q in range(N):
        for g in range(8):
            m = rng.random((16, M)) < rng.choice(np.array([0.0, 0.0, 0.06, 0.4, 1.0]), M)
            v = rng.integers(0, M, (16, M))
            if g % 2: v = rng.choice(rng.permutation(M)[:200], (16, M))
            v = np.where(rng.random((16, M)) < 0.03, np.arange(M), v); s = np.where(m, v, M)
            far = 64 + rng.permutation(M - 64); o = far[:192]; a, b, h = o[:64], o[64:128], o[128:]
            s[:, o] = M; s[5, a] = b; s[9, b] = h; s[11, b[:20]] = h[:20]; fa[q, g, h] = a; gn[q, g, h] = G0
            e = doubles(rng, far[192:384], x[q, g], s, fa[q, g], gn[q, g], g % 2 == 0)
            if g % 2:
                s[:, 32:64] = M; s[3, 32:64] = rng.choice(a, 32); s[:, 0] = M; fa[q, g, 0] = e[0]; gn[q, g, 0] = G0
            sn[q, g] = s
    return pack(x, rng.integers(0, 16, (N, 8, 16, 1)), sn, fa, gn)
def setup_inputs_spread(rng):
    sn, fa, gn = woods(rng, 9.0)
    x = (rng.random((N, 8, 16, M)) * np.exp2(8 * rng.random((N, 8, 1, M))) * (rng.random((N, 8, 1, M)) > 0.0625)).astype(np.int64)
    w = (rng.random((N, 8, 16, 1)) * np.exp2(4 * rng.random((N, 8, 16, 1)))).astype(np.int64)
    return pack(np.minimum(x, 255), np.minimum(w, 15), sn, fa, gn)
def check_inputs(d):
    bad = []
    for k, lo, hi in (("x", 0, 255), ("w", 0, 15), ("sn", 0, M), ("fa", 0, M - 1), ("gn", 0, E)):
        v = np.asarray(d[k]).astype(np.float64)
        if not (np.min(v) >= lo and np.max(v) <= hi): bad.append("range of " + k)
        elif np.any(v != np.floor(v)): bad.append("whole numbers in " + k)
    return bad
def narrow(tab, ix):
    return np.take_along_axis(tab, ix, 2)
def broad(tab, ix):
    return np.take_along_axis(tab, ix[:, :, None, :], 3)
def reference(x, w, sn, fa, gn):
    X = np.zeros((N, 8, 16, W), np.int32); X[..., :M] = x.astype(np.float32).reshape(N, 8, 16, M)
    SN = np.full((N, 8, 16, W), M, np.int64); SN[..., :M] = sn.reshape(N, 8, 16, M)
    F1 = np.zeros((N, 8, W), np.int64); F1[..., :M] = fa; F2 = F1.copy()
    GN = np.zeros((N, 8, W), np.int64); GN[..., :M] = gn
    wt = w.astype(np.float32).astype(np.int32).reshape(N, 8, 16, 1)
    ship_x = np.zeros((N, 8, 16, S), np.int32); ship_d = np.zeros((N, 8, S), np.int64); ship_h = np.full((N, 8, S), M)
    own = np.arange(L + S) < L; lower = np.tri(L, k=-1).astype(bool)
    for t in range(T):
        f = (F1 if t % 2 == 0 else F2).copy()
        order = (np.arange(W) + t * Q) % W
        ok = (np.all(SN == M, axis=2) & (GN >= G0))[..., order]; place = np.add.accumulate(ok.astype(np.int64), axis=2) - ok
        i, j, k = np.nonzero(ok & (place < L)); h = np.full((N, 8, L), M); h[i, j, place[i, j, k]] = order[k]
        xh = broad(X, h); ax = np.roll(ship_x, t, axis=0)
        xl = np.concatenate([xh, ax], axis=3); real = h != M
        live = np.concatenate([real, np.roll(ship_h, t, axis=0) != M], axis=2)
        c = np.concatenate([narrow(f, h), np.add.reduce(wt * ax, axis=2).astype(np.int64) & 63], axis=2); p = c.copy()
        b = np.concatenate([h, np.full((N, 8, S), M)], axis=2); up_n = np.ones((N, 8, L + S), np.int64)
        d = np.concatenate([np.full((N, 8, L), 2), np.roll(ship_d, t, axis=0)], axis=2)
        y = np.full((N, 8, L + S), M); s = y.copy(); a = np.zeros((N, 8, L + S), np.int64); found = np.zeros((N, 8, L + S), bool)
        for e in range(E):
            sons = broad(SN, c)
            can = (sons != M) & (sons != b[:, :, None, :])
            xs = broad(X, np.ascontiguousarray(sons.transpose(0, 1, 3, 2)).reshape(N, 8, -1)).reshape(N, 8, 16, L + S, 16)
            score = np.add.reduce(np.abs(xs - xl[..., None]), axis=2)
            best = np.argmin(np.where(can.transpose(0, 1, 3, 2), score, 2 ** 20), axis=3)
            son = np.take_along_axis(sons, best[:, :, None, :], 2)[:, :, 0]; some = np.any(can, axis=2)
            down = live & some; fail = live & ~some & (~own | (p < 64)); up = live & ~some & ~fail
            y = np.where(down, c, y); s = np.where(down, son, s); a = np.where(down, best, a); d = np.where(down, d - 1, d)
            hit = down & (d == 0); found = found | hit; live = live & ~fail & ~hit
            fp = narrow(f, p); up_n = np.where(up, up_n + 1, up_n); d = np.where(up, up_n + 1, d)
            b = np.where(up, p, np.where(down, M, b)); c = np.where(up, fp, np.where(down, son, c)); p = np.where(up, fp, p)
        fo, yo, so, ao = found[..., :L], y[..., :L], s[..., :L], a[..., :L]
        same = (yo[..., :, None] == yo[..., None, :]) | (so[..., :, None] == so[..., None, :])
        go = fo & ~np.any(same & fo[..., None, :] & lower, axis=3)
        several = np.add.reduce((broad(SN, yo) != M).astype(np.int64), axis=2) > 1
        mixed = (broad(X, so) + xh) >> 1
        back_x = np.roll(broad(X, s[..., L:]), -t, axis=0); back = np.roll(found[..., L:], -t, axis=0)
        lost = real & ~fo; place = np.add.accumulate(lost.astype(np.int64), axis=2) - lost; age = narrow(GN, h)
        i, j, k = np.nonzero(go); hh, yy, ss, aa = h[i, j, k], yo[i, j, k], so[i, j, k], ao[i, j, k]; m = several[i, j, k]
        SN[i, j, 0, hh] = ss; F2[i, j, ss] = hh; X[i, j, :, ss] = mixed[i, j, :, k]
        SN[i[m], j[m], aa[m], yy[m]] = M; F1[i[m], j[m], ss[m]] = hh[m]
        i, j, k = np.nonzero(back); hh = ship_h[i, j, k]; nc = M + 16 + S * (t - 1) + k
        X[i, j, :, nc] = back_x[i, j, :, k]; F1[i, j, nc] = hh; F2[i, j, nc] = hh; GN[i, j, nc] = GN[i, j, hh] + 1; SN[i, j, t, hh] = nc
        i, j, k = np.nonzero(lost & (place < S)); pl = place[i, j, k]
        ship_x = np.zeros((N, 8, 16, S), np.int32); ship_d = np.zeros((N, 8, S), np.int64); ship_h = np.full((N, 8, S), M)
        ship_x[i, j, :, pl] = xh[i, j, :, k]; ship_d[i, j, pl] = age[i, j, k]; ship_h[i, j, pl] = h[i, j, k]
    return {"xo": X.reshape(N, 128, W).astype(np.float32).astype(BF), "fo": F1.astype(np.float32), "f2o": F2.astype(np.float32)}

@@ -1,0 +1,784 @@
+import numpy as np
+from concourse.mybir import dt, AluOpType, AxisListType, ActivationFunctionType
+
+M, L, S, NE, NT, W = 3264, 96, 32, 5, 4, 3376
+NB = 211
+XWW, FGWW = W + 96, W + 96
+SNWW = W + 96 + 96 + 32
+BADW = W + 96 + 96 + 32
+SEG = 17
+NSEG = 8 * SEG
+BIGX = 4096.0
+NENG = 8
+CH = {"A": (("s", 24), ("v", 40), ("v", 32)), "B": (("s", 24), ("v", 40), ("v", 32)), "R": (("s", 16), ("v", 16))}
+AV = {"A": 6, "B": 2, "R": 0}
+NR = {"A": "s", "B": "v", "R": "s"}
+GQ = [4]
+OPT = {"slack": 0.0, "pe": 0.0006, "bias": {}}
+WAKE = 0.12
+
+SCRATCH, VS, PHYS = {}, {}, {}
+
+
+def _d(name, cols, dtype="float32", where="sbuf", rows=128):
+    VS[name] = (where, [rows, cols], dtype)
+    if where == "sbuf" and cols < 2000 and not name[:2] in ("MB", "AR", "RB", "RR"):
+        pool = "pool_" + dtype
+        at = SCRATCH[pool][1][1] if pool in SCRATCH else 0
+        PHYS[name] = (pool, at)
+        SCRATCH[pool] = ("sbuf", [128, at + (cols + 15) // 16 * 16], dtype)
+    else:
+        PHYS[name] = (name, 0)
+        SCRATCH[name] = (where, [rows, cols], dtype)
+
+
+for _n, _c, _t in (("SNW", SNWW, "int32"), ("XW", XWW, "bfloat16"), ("FGW", FGWW, "float32"), ("BAD", BADW, "bfloat16"),
+                   ("GD", 204, "int32"), ("FD", 204, "int32"), ("GDB", 204, "bfloat16"), ("GDF", 204, "float32"), ("FDF", 204, "float32"),
+                   ("GB8", M, "bfloat16"), ("WC", 1, "bfloat16"), ("NGB", 212, "float32"),
+                   ("OKR", 212, "bfloat16"), ("CUM", NB, "float32"), ("SJ", 6 * NB, "bfloat16"), ("HR", 8, "float32"), ("RHO", 8, "uint16"),
+                   ("RK", 212, "float32"), ("RG", 96, "float32"), ("VG", 96, "float32"), ("HV", 96, "float32"),
+                   ("HREP", 96, "float32"), ("PREP", 96, "float32"), ("FH", 96, "float32"), ("FP", 96, "float32"),
+                   ("XL", 96, "bfloat16"), ("XLE", 1536, "bfloat16"), ("XLR", 512, "bfloat16"),
+                   ("DGM", 3 * 192, "float32"), ("DGS", 3 * 192, "float32"), ("HW", 8, "float32"), ("PWF", 8, "float32"),
+                   ("LU", 64, "uint16"),
+                   ("IT", 8, "int32"), ("COL", 16, "float32"), ("CI", 192, "int32"), ("CJ", 192, "int32"), ("C128", 192, "float32"), ("CHI", 144, "float32"), ("CLO", 192, "float32"),
+                   ("J", NSEG, "float32"), ("T1", 144, "float32"), ("T2", 144, "float32"),
+                   ("ONEF", 128, "float32"), ("ONEB", 128, "bfloat16"), ("BLK", 8, "bfloat16"), ("TRIN", 128, "bfloat16"), ("ZW", 144, "bfloat16"), ("Z8", 144, "bfloat16"),
+                   ("SEL0", 128, "float32"), ("SEL1", 128, "float32"), ("SEL2", 128, "bfloat16"), ("MASK", 192, "float32"), ("BL", 8, "float32"), ("IDF", 128, "float32"),
+                   ("PERF", NSEG, "float32"), ("PERB", NSEG, "bfloat16"), ("CK", NSEG, "bfloat16"), ("CP1", NSEG, "float32"), ("CP2", NSEG, "float32"),
+                   ("O1B", 128, "bfloat16"), ("O1F", 216, "float32"), ("RST", NSEG, "float32"), ("KB", 8, "float32"), ("KROW", 96, "float32"),
+                   ("VAL0", 216, "float32"), ("VAL1", 216, "float32"), ("VAL2", 216, "float32"), ("VAL3", 216, "float32"),
+                   ("LW", 8, "float32"), ("DUM", 18, "float32"), ("DS1", 8, "float32"), ("DUMR", 32, "float32"), ("DUMW", 8, "float32"), ("RS16", 192, "float32"), ("TRIM", 96, "float32"),
+                   ("NC", 96, "float32"), ("WB", 128, "bfloat16"), ("BLQ", 8, "float32"), ("IDB", 128, "bfloat16"), ("IDN", 128, "bfloat16"), ("O64", 128, "float32"), ("RSM", NSEG, "float32"),
+                   ("W6", 192, "float32"), ("I6", 24, "int32"), ("EXY", 96, "float32"), ("EXS", 96, "float32"), ("EXA", 96, "bfloat16"),
+                   ("EQP", 960, "bfloat16"), ("EQM", 192, "bfloat16"), ("FR", 96, "float32"), ("ADB", 192, "float32"), ("SY", 96, "float32"), ("NEY", 96, "bfloat16"), ("SEV", 96, "float32"),
+                   ("XS", 96, "bfloat16"), ("XI", 192, "int32"), ("FS", 96, "float32"), ("FM", 96, "float32"), ("FDL", 96, "float32"),
+                   ("NHF", 96, "float32"), ("NHY", 192, "int32"), ("SLM", 96, "float32"), ("GY", 96, "float32"), ("LS6", 8, "bfloat16"), ("FN1", 96, "float32"), ("FN2", 96, "float32"),
+                   ("RI", 32, "int32"), ("RI2", 32, "int32"), ("RW", 32, "float32"), ("FL", 32, "float32"), ("HPD", 32, "float32"), ("CUR", 32, "float32"), ("CUR2", 32, "int32"), ("FLN", 32, "float32")):
+    _d(_n, _c, _t)
+for _t in range(3):
+    _d("MB%d" % _t, 160, "bfloat16")
+    _d("FNW%d" % _t, 128, "float32")
+    _d("AR%d" % (_t + 1), 64, "bfloat16")
+    _d("RB%d" % (_t + 1), 32, "bfloat16")
+    _d("RR%d" % (_t + 1), 32, "bfloat16")
+for _c, _n in (("A", 96), ("B", 96), ("R", 32)):
+    _d("SF" + _c, _n), _d("SU" + _c, _n, "uint16"), _d("DD" + _c, 16 * _n, "bfloat16"), _d("EQ" + _c, _n, "bfloat16")
+    _d("WK" + _c, 5 * NSEG), _d("AA" + _c, 128)
+for _t in range(8):
+    _d("P%d" % _t, 512, "float32", "psum")
+_d("DGB", M, "bfloat16", "dram", 8)
+_d("DGF", M, "float32", "dram", 8)
+_d("DFF", M, "float32", "dram", 8)
+
+_DMAS = ["sn0", "sn1", "sn2", "sn3", "xin", "gin", "fin", "win", "gb1", "gb2", "ff1", "ff2", "ff3", "gf1", "gf2", "o1", "o2", "o3"]
+SEMAPHORES = ["sv", "ss", "st", "sg", "ls"] + ["d_" + n for n in _DMAS] + ["ar%d" % t for t in (1, 2, 3)] + ["rr%d" % t for t in (1, 2, 3)]
+
+ADD, SUB, MUL, MAX, MIN = AluOpType.add, AluOpType.subtract, AluOpType.mult, AluOpType.max, AluOpType.min
+EQ, NEQ, LT, GE, GT, LE = AluOpType.is_equal, AluOpType.not_equal, AluOpType.is_lt, AluOpType.is_ge, AluOpType.is_gt, AluOpType.is_le
+AF = ActivationFunctionType
+
+
+def R(buf, a=0, b=None, step=1, p0=0, p1=None, ps=1):
+    rows, cols = VS[buf][1]
+    return (buf, a, cols if b is None else b, step, p0, rows if p1 is None else p1, ps)
+
+
+def ap(T, r):
+    n, o = PHYS[r[0]]
+    if r[3] == 1 and r[6] == 1:
+        return T[n][r[4]:r[5], o + r[1]:o + r[2]]
+    return T[n][r[4]:r[5]:r[6], o + r[1]:o + r[2]:r[3]]
+
+
+def wid(r):
+    return (r[2] - r[1] + r[3] - 1) // r[3]
+
+
+def _hit1(a0, a1, s, b0, b1, u):
+    if a1 <= b0 or b1 <= a0:
+        return False
+    return not (s == u and s > 1 and (a0 - b0) % s)
+
+
+def hit(x, y):
+    return x[0] == y[0] and _hit1(x[1], x[2], x[3], y[1], y[2], y[3]) and _hit1(x[4], x[5], x[6], y[4], y[5], y[6])
+
+
+def is_ps(r):
+    return VS[r[0]][0] == "psum"
+
+
+CY = 0.00083
+OPS = []
+
+
+def op(q, fn, rd, wr, cost, tail=0.0, sem=None, n=1, count=1):
+    OPS.append({"q": q, "fn": fn, "rd": [r for r in rd if r], "wr": wr, "cost": cost, "tail": tail, "sem": sem, "n": n, "count": count, "i": len(OPS)})
+
+
+def two(*rs):
+    return all(VS[r[0]][2] in ("bfloat16", "uint16") for r in rs)
+
+
+def _isr(s):
+    return s if isinstance(s, tuple) else None
+
+
+def cp(out, a):
+    op("v", lambda g, T: g.vector.tensor_copy(ap(T, out), ap(T, a)), [a], [out], max(64, wid(a) * (0.5 if two(out, a) else 1)) * CY)
+
+
+def gat(out, win, off, q="v"):
+    if q == "v":
+        op("v", lambda g, T: g.vector.tensor_copy(ap(T, out), ap(T, win).indirect(ap(T, off))), [win, off], [out], 0.05 + wid(out) * 1.56 * CY)
+    else:
+        op("s", lambda g, T: g.scalar.activation(ap(T, out), ap(T, win).indirect(ap(T, off)), AF.Copy), [win, off], [out], 0.065 + wid(out) * 1.56 * CY)
+
+
+def gsub(out, win, off, b):
+    op("v", lambda g, T: g.vector.tensor_tensor(ap(T, out), ap(T, win).indirect(ap(T, off)), ap(T, b), SUB), [win, off, b], [out], 0.05 + wid(out) * 1.56 * CY)
+
+
+def scat(win, off, a):
+    op("v", lambda g, T: g.vector.tensor_copy(ap(T, win).indirect(ap(T, off)), ap(T, a)), [a, off], [win], 0.05 + wid(a) * 3 * CY)
+
+
+def tt(out, a, b, o):
+    op("v", lambda g, T: g.vector.tensor_tensor(ap(T, out), ap(T, a), ap(T, b), o), [a, b], [out], max(64, wid(a) * (1 if is_ps(a) or is_ps(b) else 2)) * CY)
+
+
+def ts(out, a, s1, s2, o0, o1=None):
+    def fn(g, T):
+        x1 = ap(T, s1) if isinstance(s1, tuple) else s1
+        x2 = ap(T, s2) if isinstance(s2, tuple) else s2
+        if o1 is None:
+            return g.vector.tensor_scalar(ap(T, out), ap(T, a), x1, None, o0)
+        return g.vector.tensor_scalar(ap(T, out), ap(T, a), x1, x2, o0, o1)
+    op("v", fn, [a, _isr(s1), _isr(s2)], [out], max(64, wid(a) * (0.5 if two(out, a) else 1)) * CY)
+
+
+def scan(out, d0, d1, init, o0, o1):
+    op("v", lambda g, T: g.vector.tensor_tensor_scan(ap(T, out), ap(T, d0), ap(T, d1), init, o0, o1), [d0, d1], [out], max(64, wid(out)) * CY)
+
+
+def fill(out, c):
+    op("v", lambda g, T: g.vector.memset(ap(T, out), c), [], [out], max(64, wid(out) * (0.5 if two(out) else 1)) * CY)
+
+
+def act(out, a, f=None, scale=1.0, bias=0.0, acc=None):
+    def fn(g, T):
+        kw = {}
+        if isinstance(scale, tuple):
+            kw["scale"] = ap(T, scale)
+        elif scale != 1.0:
+            kw["scale"] = scale
+        if isinstance(bias, tuple):
+            kw["bias"] = ap(T, bias)
+        elif bias != 0.0:
+            kw["bias"] = bias
+        if acc:
+            kw["accum_out"] = ap(T, acc)
+        return g.scalar.activation(ap(T, out), ap(T, a), f or AF.Copy, **kw)
+    op("s", fn, [a, _isr(scale), _isr(bias)], [out] + ([acc] if acc else []), 0.06 + wid(a) * CY)
+
+
+def mm(group):
+    mms([group])
+
+
+def mms(groups):
+    rd, wr, cost = [], [gr[0][0] for gr in groups], 0.0
+    for gr in groups:
+        for o, l, r in gr:
+            for x in (l, r):
+                if x not in rd:
+                    rd.append(x)
+            cost += max(min(64, wid(l)), wid(r)) * (1 if two(l) else 4) * 0.0006
+
+    def fn(g, T):
+        return [g.tensor.matmul(ap(T, o), ap(T, l), ap(T, r), k == 0, k == len(gr) - 1) for gr in groups for k, (o, l, r) in enumerate(gr)]
+    op("t", fn, rd, wr, cost)
+
+
+def iota(out, pat, base, cm):
+    kw = {} if VS[out[0]][2] == "int32" else {"allow_small_or_imprecise_dtypes": True}
+    op("g", lambda g, T: g.iota(ap(T, out), pat, base, cm, **kw), [], [out], 0.13 + 2 * wid(out) * CY)
+
+
+def dma(q, sem, out, a, oap=None, aap=None, us=2.0):
+    def fn(g, T):
+        e = g.sync if q == "y" else g.scalar
+        return e.dma_start(oap(T) if oap else ap(T, out), aap(T) if aap else ap(T, a))
+    op(q, fn, [a], [out] if out else [], 0.1, us, "d_" + sem, 16)
+
+
+def consts():
+    iota(R("IT", 0, 1), [[0, 1]], 0, 1)
+    iota(R("CI"), [[1, 192]], 0, 0)
+    iota(R("C128"), [[1, 192]], 0, 0)
+    iota(R("J"), [[0, 8], [1, SEG]], 0, 0)
+    ts(R("IT", 1, 2), R("IT", 0, 1), 15, None, AluOpType.bitwise_and)
+    ts(R("IT", 2, 3), R("IT", 0, 1), 4, None, AluOpType.arith_shift_right)
+    cp(R("COL", 0, 3), R("IT", 0, 3))
+    P, PLO, PHI = R("COL", 0, 1), R("COL", 1, 2), R("COL", 2, 3)
+    tt(R("COL", 3, 4), P, PHI, ADD)
+    ts(R("COL", 4, 5), PHI, 16.0, 15.0, MUL, ADD)
+    ts(R("COL", 5, 6), P, 16.0, 15.0, MUL, ADD)
+    for k in range(4):
+        ts(R("COL", 6 + k, 7 + k), PLO, float(k), None, EQ)
+    ts(R("COL", 10, 11), PLO, 1.5, None, LT)
+    ts(R("CJ"), R("CI"), 15, None, AluOpType.bitwise_and)
+    cp(R("CLO"), R("CJ"))
+    ts(R("XI", 0, 144), R("CI", 0, 144), 4, None, AluOpType.arith_shift_right)
+    cp(R("CHI"), R("XI", 0, 144))
+    ts(R("ONEF"), R("CHI", 0, 128), PHI, None, EQ)
+    ts(R("ONEB"), R("CHI", 0, 128), PHI, None, EQ)
+    ts(R("BLK"), R("C128", 0, 8), PHI, 16.0, EQ, MUL)
+    ts(R("BL"), R("C128", 0, 8), PHI, None, EQ)
+    ts(R("T1", 0, 128), R("CLO", 0, 128), PLO, -1.0, LT, MUL)
+    tt(R("TRIN"), R("T1", 0, 128), R("ONEF"), MUL)
+    ts(R("ZW"), R("C128", 0, 144), R("COL", 4, 5), None, EQ)
+    ts(R("Z8"), R("C128", 0, 144), R("COL", 5, 6), None, EQ)
+    for k in range(3):
+        ts(R("SEL%d" % k), R("ONEF"), R("COL", 6 + k, 7 + k), None, MUL)
+    ts(R("MASK"), R("CLO"), PLO, None, EQ)
+    ts(R("IDF"), R("C128", 0, 128), P, None, EQ)
+    ts(R("IDB"), R("C128", 0, 128), P, None, EQ)
+    ts(R("IDN"), R("C128", 0, 128), P, -1.0, EQ, MUL)
+    ts(R("IT", 3, 4), R("IT", 2, 3), 1, None, AluOpType.bitwise_and)
+    cp(R("COL", 11, 12), R("IT", 3, 4))
+    ts(R("BLQ"), R("C128", 0, 8), R("COL", 11, 12), None, EQ)
+    fill(R("O64"), 3264.0)
+    ts(R("T2", 0, NSEG), R("C128", 0, NSEG), -1.0, None, ADD)
+    ts(R("PERF"), R("T2", 0, NSEG), R("COL", 3, 4), None, EQ)
+    ts(R("PERB"), R("PERF"), 262144.0, None, MUL)
+    ts(R("RST"), R("J"), 0.0, 2e9, EQ, MUL)
+    ts(R("RST"), R("RST"), -1e9, None, ADD)
+    ts(R("CP1"), R("J"), 0.0, 3264.0, EQ, MUL)
+    ts(R("T1", 0, NSEG), R("J"), -1.0, 0.0, ADD, MAX)
+    ts(R("COL", 12, 13), PLO, 1.0, None, ADD)
+    ts(R("RSM"), R("J"), 0.5, None, GT)
+    ts(R("T2", 0, NSEG), R("J"), 4096.0, None, MUL)
+    tt(R("CP2"), R("T2", 0, NSEG), R("CP1"), ADD)
+    ts(R("T2", 0, NSEG), R("J"), 0.0, 131072.0, EQ, MUL)
+    tt(R("CK"), R("T1", 0, NSEG), R("T2", 0, NSEG), ADD)
+    fill(R("O1B"), 1.0)
+    fill(R("O1F"), 1.0)
+    ts(R("LW", 0, 6), R("C128", 0, 6), 16.0, PLO, MUL, ADD)
+    ts(R("KB", 0, 6), R("LW", 0, 6), 0.5, None, ADD)
+    ts(R("KROW"), R("C128", 0, 96), 1.0, None, ADD)
+    for k in range(3):
+        ts(R("DUM", 6 * k, 6 * k + 6), R("LW", 0, 6), float(W + (96 if k == 1 else 0)), None, ADD)
+    ts(R("DS1", 0, 6), R("LW", 0, 6), 33.0, None, ADD)
+    ts(R("DUMR"), R("C128", 0, 32), float(W + 192), None, ADD)
+    ts(R("DUMW", 0, 2), R("LW", 0, 2), float(W + 192), None, ADD)
+    ts(R("RS16"), R("CLO"), 0.5, None, GT)
+    ts(R("TRIM"), R("CLO", 0, 96), PLO, 20000.0, LE, MUL)
+    for t in range(1, 4):
+        ts(R("NC", 32 * t - 32, 32 * t), R("C128", 0, 32), float(16 + 32 * (t - 1)), R("COL", 6 + t, 7 + t), ADD, MUL)
+    for t in range(4):
+        s = 66 * t
+        iota(R("VAL%d" % t, 0, NB - s), [[16, NB - s]], 16 * s - M, 0)
+        if s:
+            iota(R("VAL%d" % t, NB - s, NB), [[16, s]], -M, 0)
+        iota(R("VAL%d" % t, NB, 216), [[0, 216 - NB]], 0, 0)
+        ts(R("VAL%d" % t), R("VAL%d" % t), PLO, None, ADD)
+    fill(R("P2", 0, 2 * NSEG), 0.0)
+    fill(R("RK", NB, 212), 0.0)
+    fill(R("OKR", NB, 212), 0.0)
+    fill(R("NGB", 204, 212), 0.0)
+    for t in range(3):
+        fill(R("MB%d" % t), 0.0)
+        fill(R("FNW%d" % t), 0.0)
+
+
+def load():
+    dma("y", "gin", R("GD"), None, aap=lambda T: T.gn[:, :], us=2.5)
+    dma("a", "fin", R("FD"), None, aap=lambda T: T.fa[:, :], us=2.5)
+    c = M // 4
+    for k in range(4):
+        dma("y", "sn%d" % k, R("SNW", c * k, c * k + c), None, aap=lambda T, k=k: T.sn[:, c * k:c * k + c], us=3.0 + 1.5 * k)
+    dma("a", "win", R("WC"), None, aap=lambda T: T.w[:, :], us=2.0)
+    dma("a", "xin", R("XW", 0, M), None, aap=lambda T: T.x[:, :], us=9.0)
+    iota(R("FGW"), [[0, FGWW]], 0, 0)
+    ts(R("GDB"), R("GD"), 3.0, None, LT)
+    cp(R("GDF"), R("GD"))
+    cp(R("FDF"), R("FD"))
+    wh = lambda n: (n, 0, M, 1, 0, 8, 1)
+    dma("a", "gb1", wh("DGB"), R("GDB"))
+    dma("a", "ff1", wh("DFF"), R("FDF"))
+    dma("a", "gf1", wh("DGF"), R("GDF"))
+    dma("a", "gb2", R("GB8", p1=8), wh("DGB"))
+    dma("a", "ff2", R("FGW", 0, M, p0=0, ps=16), wh("DFF"))
+    dma("a", "ff3", R("FGW", 0, M, p0=1, ps=16), wh("DFF"))
+    dma("a", "gf2", R("FGW", 0, M, p0=2, ps=16), wh("DGF"))
+    fill(R("SNW", M, SNWW), 3264)
+    fill(R("XW", M, M + 16), BIGX)
+    fill(R("XW", M + 16, XWW), 0.0)
+    fill(R("BAD", M, BADW), 1.0)
+
+
+def load2():
+    c = M // 4
+    for k in range(4):
+        ts(R("BAD", c * k, c * k + c), R("SNW", c * k, c * k + c), 3264.0, None, NEQ)
+    mm([(R("P3", 0, 204), R("Z8", 15 - lo, 143 - lo, p1=8), R("GB8", lo, M, 16, p1=8)) for lo in range(16)])
+    ts(R("NGB", 0, 204), R("P3", 0, 204), -1.0, None, MUL)
+    ts(R("WB"), R("ONEB"), R("WC"), None, MUL)
+
+
+def diag(src, n, k, msk=True):
+    m, s = R("DGM", 192 * k, 192 * k + n), R("DGS", 192 * k, 192 * k + n)
+    tt(m, src, R("MASK", 0, n), MUL)
+    scan(s, R("RS16", 0, n), m, 0.0, MUL, ADD)
+    return R("DGS", 192 * k + 15, 192 * k + n, 16)
+
+
+def level(ch, bank, nl, off, bar, xle, last):
+    kc = nl // 16
+    sf, su, dd = R("SF" + ch), R("SU" + ch), "DD" + ch
+    gat(sf, R("SNW", 0, W), off)
+    cp(su, sf)
+    cpr = R("CP2" if last else "CP1", p1=1)
+    pt, pk, pw = R(bank, 0, NSEG, p1=nl), R(bank, NSEG, 2 * NSEG, p1=nl), R(bank, 300, 300 + kc)
+    mm([(pt, R("O1F", 0, nl, p1=1), cpr), (pt, sf, R("PERF"))])
+    keys = [(pk, R("O1B", 0, nl, p1=1), R("CK", p1=1))]
+    if bar:
+        tt(R("EQ" + ch), sf, bar, EQ)
+        keys.append((pk, R("EQ" + ch), R("PERB")))
+    differences(ch, dd, xle)
+    for s in range(16):
+        keys.append((R(bank, NSEG + 1 + s, 2 * NSEG, SEG, p1=nl), R(dd, s, 16 * nl, 16), R("BLK")))
+    mm(keys)
+    argmin(ch, pk, pt, nl, 8, last)
+    mm([(pw, R("AA" + ch, p1=nl), R("BL", 0, kc, p1=nl))])
+    return pw
+
+
+def differences(ch, dd, xle):
+    at = 0
+    for e, n in CH[ch]:
+        a, b = 16 * at, 16 * (at + n)
+        if e == "v":
+            gsub(R(dd, a, b), R("XW", 0, W), R("SU" + ch, at, at + n), R(xle, a, b))
+            act(R(dd, a, b), R(dd, a, b), AF.Abs)
+        else:
+            gat(R(dd, a, b), R("XW", 0, W), R("SU" + ch, at, at + n), "s")
+            ps = R("P7" if ch == "R" else "P5", 0, b - a)
+            mm([(ps, R("IDB"), R(dd, a, b)), (ps, R("IDN"), R(xle, a, b))])
+            act(R(dd, a, b), ps, AF.Abs)
+        at += n
+
+
+def argmin(ch, pk, pt, np_, ns, last=False):
+    k = SEG * ns
+    wk = [R("WK" + ch, NSEG * j, NSEG * j + k, p1=np_) for j in range(5)]
+    scan(wk[0], R("RST", 0, k, p1=np_), pk, 0.0, MAX, MIN)
+    tt(wk[1], pk, wk[0], EQ)
+    if last:
+        tt(wk[3], wk[1], pt, MUL)
+        scan(wk[4], R("RSM", 0, k, p1=np_), wk[3], 0.0, MUL, MAX)
+    else:
+        if NR[ch] == "s":
+            act(wk[2], wk[1], AF.Copy, scale=-1.0, bias=1.0)
+        else:
+            ts(wk[2], wk[1], -1.0, 1.0, MUL, ADD)
+        tt(wk[3], wk[1], pt, MUL)
+        scan(wk[4], wk[2], wk[3], 0.0, MUL, ADD)
+    for gi in range(ns):
+        o, z = R("AA" + ch, 16 * gi, 16 * gi + 16, p1=np_), 4 * NSEG + SEG * gi + 16
+        if gi < ns - AV[ch]:
+            act(o, R("MASK", 0, 16, p1=np_), AF.Copy, scale=R("WK" + ch, z, z + 1, p1=np_))
+        else:
+            ts(o, R("MASK", 0, 16, p1=np_), R("WK" + ch, z, z + 1, p1=np_), None, MUL)
+
+
+def guest_level(off):
+    sf, su, dd = R("SFR"), R("SUR"), "DDR"
+    gat(sf, R("SNW", 0, W), off)
+    cp(su, sf)
+    differences("R", dd, "XLR")
+    n = GQ[0]
+    qs = [(q, {"p0": 16 * n * q, "p1": 16 * n * q + 32}) for q in range(8 // n)]
+    k = n * SEG
+    mms([[(R("P2", 0, k, **p), R("O1F", 0, 32, p1=1), R("CP1", 0, k, p1=1)), (R("P2", 0, k, **p), sf, R("PERF", k * q, k * q + k))] for q, p in qs])
+    mms([[(R("P2", k, 2 * k, **p), R("O1B", 0, 32, p1=1), R("CK", 0, k, p1=1))]
+         + [(R("P2", k + 1 + s, 2 * k, SEG, **p), R(dd, s, 512, 16), R("BLK", n * q, n * q + n)) for s in range(16)] for q, p in qs])
+    argmin("R", R("P2", k, 2 * k), R("P2", 0, k), 128, n)
+    mms([[(R("P2", 300, 302, p0=p["p0"], p1=p["p0"] + 16 * n), R("AAR", 0, 16 * n, **p), R("BLQ", 0, 2, **p))] for q, p in qs])
+    return R("P2", 300, 302)
+
+
+def arrivals(t):
+    ar = "AR%d" % t
+    op("n", None, [R("MB%d" % (t - 1), 0, 64)], [R(ar)], 0.0, 3.0, "ar%d" % t, NENG)
+    for k in range(16):
+        act(R("XLR", k, 512, 16), R(ar, 32, 64))
+    mm([(R("P2", 310, 342), R("WB"), R(ar, 32, 64))])
+    mm([(R("P2", 342, 374), R("SEL2"), R(ar, 0, 32))])
+    cp(R("RI"), R("P2", 310, 342))
+    ts(R("RI2"), R("RI"), 63, None, AluOpType.bitwise_and)
+    tt(R("DGM", 384, 416), R("RI2"), R("MASK", 0, 32), MUL)
+    tt(R("DGM", 416, 448), R("P2", 342, 374), R("MASK", 0, 32), MUL)
+    scan(R("DGS", 384, 448), R("RS16", 0, 64), R("DGM", 384, 448), 0.0, MUL, ADD)
+    cp(R("LU", 32, 34), R("DGS", 384 + 15, 416, 16))
+    cp(R("RW", 0, 2), R("DGS", 416 + 15, 448, 16))
+    for k in (3, 4, 5):
+        ts(R("RW", 2 * k, 2 * k + 2), R("RW", 0, 2), float(k + 1), None, EQ)
+    for k in range(1, 6):
+        pw = guest_level(R("LU", 32 + 2 * k - 2, 32 + 2 * k))
+        if k < 5:
+            cp(R("LU", 32 + 2 * k, 34 + 2 * k), pw)
+        if k >= 3:
+            ts(R("RW", 12, 14), pw, -3264.0, None, ADD)
+            tt(R("RW", 14 + 2 * k, 16 + 2 * k), R("RW", 12, 14), R("RW", 2 * k, 2 * k + 2), MUL)
+            if k == 4:
+                tt(R("RW", 26, 28), R("RW", 20, 22), R("RW", 22, 24), ADD)
+    tt(R("RW", 28, 30), R("RW", 26, 28), R("RW", 24, 26), ADD)
+    ts(R("LU", 42, 44), R("RW", 28, 30), 3264.0, None, ADD)
+    gat(R("RB%d" % t), R("XW", 0, W), R("LU", 42, 44))
+    op("g", ("ret", t), [R("RB%d" % t)], [], 0.6, 1.0, "ls", NENG)
+
+
+def lanes(t):
+    mm([(R("P3", 0, NB), R("ZW", 15 - lo, 143 - lo), R("BAD", lo, W, 16)) for lo in range(16)])
+    s = 66 * t
+    tt(R("OKR", 0, NB - s), R("P3", s, NB), R("NGB", s, NB), EQ)
+    if s:
+        tt(R("OKR", NB - s, NB), R("P3", 0, s), R("NGB", 0, s), EQ)
+    tot, pre = R("P3", 256, 256 + NB), R("P3", 0, NB)
+    mm([(tot, R("ONEB"), R("OKR", 0, NB))])
+    mm([(pre, R("TRIN"), R("OKR", 0, NB))])
+    scan(R("CUM"), R("O1F", 0, NB), tot, 0.0, MUL, ADD)
+    for k in range(6):
+        act(R("SJ", NB * k, NB * k + NB), R("CUM"), AF.Sign, scale=-1.0, bias=R("KB", k, k + 1), acc=R("HR", k, k + 1))
+    tt(R("RK", 0, NB), R("CUM"), pre, ADD)
+    tt(R("RK", 0, NB), R("RK", 0, NB), R("OKR", 0, NB), MUL)
+    ts(R("RHO", 0, 6), R("HR", 0, 6), 0.5, NB / 2, MUL, ADD)
+    gat(R("VG"), R("VAL%d" % t, 0, 212), R("RHO", 0, 6), "s")
+    gat(R("RG"), R("RK"), R("RHO", 0, 6))
+    tt(R("RG"), R("RG"), R("KROW"), EQ)
+    tt(R("HV"), R("RG"), R("VG"), MUL)
+    mm([(R("P4", 0, 96), R("O64", p1=1), R("O1F", 0, 96, p1=1)), (R("P4", 0, 96), R("ONEF"), R("HV"))])
+    hs = diag(R("P4", 0, 96), 96, 0)
+    cp(R("LU", 0, 6), hs)
+    act(R("HREP"), R("P4", 0, 96))
+    act(R("HW", 0, 6), hs)
+    gat(R("FH"), R("FGW", 0, W), R("LU", 0, 6))
+    gat(R("XL"), R("XW", 0, W), R("LU", 0, 6))
+    for k in range(16):
+        if k % 2:
+            act(R("XLE", k, 1536, 16), R("XL"))
+        else:
+            cp(R("XLE", k, 1536, 16), R("XL"))
+    sel = R("SEL%d" % (t % 2))
+    mm([(R("P4", 96, 192), sel, R("FH"))])
+    ps = diag(R("P4", 96, 192), 96, 1)
+    cp(R("LU", 6, 12), ps)
+    act(R("PWF", 0, 6), ps)
+    gat(R("FP"), R("FGW", 0, W), R("LU", 6, 12))
+    mm([(R("P4", 192, 288), sel, R("FP"))])
+    cp(R("LU", 12, 18), diag(R("P4", 192, 288), 96, 0))
+
+
+def w6(k, n=6):
+    return R("W6", 6 * k, 6 * k + n)
+
+
+def own(t):
+    pa = level("A", "P0", 96, R("LU", 6, 12), R("P4", 0, 96), "XLE", False)
+    cp(R("LU", 18, 24), pa)
+    act(w6(1), pa)
+    pb = level("B", "P1", 96, R("LU", 12, 18), R("P4", 96, 192), "XLE", False)
+    cp(R("LU", 24, 30), pb)
+    pa = level("A", "P0", 96, R("LU", 18, 24), None, "XLE", True)
+    act(w6(0), pa)
+    pb = level("B", "P1", 96, R("LU", 24, 30), None, "XLE", False)
+    cp(R("LU", 46, 52), pb)
+    act(w6(3), pb)
+    pb = level("B", "P1", 96, R("LU", 46, 52), None, "XLE", True)
+    ts(w6(7), R("HW", 0, 6), 3264.0, None, NEQ)
+    ts(w6(9), R("PWF", 0, 6), 64.0, None, GE)
+    tt(w6(9), w6(9), w6(7), MUL)
+    ts(w6(4), w6(0), 3264.0, None, NEQ)
+    ts(w6(5), w6(0), 3264.0, None, EQ)
+    tt(w6(11), w6(4), w6(7), MUL)
+    tt(w6(23), w6(9), w6(5), MUL)
+    tt(w6(24), w6(4), w6(0), MUL)
+    tt(w6(25), w6(4), w6(1), MUL)
+    tt(w6(8), w6(5), w6(3), MUL)
+    tt(w6(8), w6(8), w6(25), ADD)
+    ts(w6(26), w6(8), 5.0, None, ADD)
+    ts(w6(25), w6(8), 10005.0, None, ADD)
+    ts(w6(6), pb, 3264.0, None, NEQ)
+    tt(w6(6), w6(6), w6(23), MUL)
+    tt(w6(10), w6(6), w6(11), ADD)
+    tt(w6(28), pb, w6(5), MUL)
+    tt(R("I6", 0, 6), w6(28), w6(24), ADD)
+    ts(R("I6", 6, 12), R("I6", 0, 6), 4095, None, AluOpType.bitwise_and)
+    ts(R("I6", 12, 18), R("I6", 0, 6), 12, None, AluOpType.arith_shift_right)
+    cp(R("LU", 52, 58), R("I6", 6, 12))
+    cp(R("LU", 58, 64), w6(8))
+    if t < 3:
+        send(t)
+    cp(w6(12, 12), R("I6", 6, 18))
+    ts(w6(27), R("I6", 6, 12), 5.0, None, ADD)
+    ts(w6(14), w6(10), -10000.0, None, MUL)
+    tt(w6(14), w6(14), w6(25), ADD)
+    tt(w6(15), w6(26), w6(10), MUL)
+    tt(w6(16), w6(27), w6(10), MUL)
+    for b, k, q in (("EXY", 14, 0), ("EXS", 27, 1), ("EXA", 13, 1)):
+        for l in range(6):
+            o, sc = R(b, 16 * l, 16 * l + 16), R("W6", 6 * k + l, 6 * k + l + 1)
+            if q:
+                act(o, R("MASK", 0, 16), AF.Copy, scale=sc)
+            else:
+                ts(o, R("MASK", 0, 16), sc, None, MUL)
+    yr, sr, ym, sm = [R("P6", 96 * k, 96 * k + 96) for k in range(4)]
+    mm([(yr, R("ONEF"), R("EXY"))])
+    mm([(sr, R("ONEF"), R("EXS"))])
+    mm([(ym, R("ONEF"), R("EXY")), (ym, R("IDF"), R("TRIM"))])
+    mm([(sm, R("ONEF"), R("EXS")), (sm, R("IDF"), R("TRIM"))])
+    ar = R("P4", 288, 384)
+    mm([(ar, R("ONEB"), R("EXA"))])
+    cf = []
+    for v in range(2):
+        for l in range(6):
+            sc = R("W6", 6 * (15 + v) + l, 6 * (15 + v) + l + 1)
+            b = 192 + 96 * v + 16 * l
+            ts(R("EQM", 96 * v + 16 * l, 96 * v + 16 * l + 16), R("P6", b, b + 16), sc, None, EQ)
+            if l < 5:
+                n, e = 80 - 16 * l, 480 * v + 96 * l
+                ts(R("EQP", e, e + n), R("P6", 96 * v + 16 * l + 16, 96 * v + 96), sc, None, EQ)
+                cf.append((R("P4", 384 + 16 * l + 16, 480), R("ONEB"), R("EQP", e, e + n)))
+    cfl = R("P4", 384, 480)
+    mm([(cfl, R("ONEB"), R("EQM", 0, 96))] + cf + [(cfl, R("ONEB"), R("EQM", 96, 192))])
+    gat(R("SY"), R("SNW", 0, W), R("LU", 58, 64))
+    ts(R("NEY"), R("SY"), 3264.0, None, NEQ)
+    sv = R("P4", 192, 288)
+    mm([(sv, R("ONEB"), R("NEY"))])
+    ts(R("SEV"), sv, 1.5, None, GT)
+    ts(R("FR"), yr, 9000.0, None, LT)
+    tt(R("FR"), R("FR"), R("MASK", 0, 96), MUL)
+    tt(R("ADB", 0, 96), cfl, R("FR"), LT)
+    tt(R("ADB", 96, 192), R("ADB", 0, 96), R("SEV"), MUL)
+    scan(R("DGS", 0, 192), R("RS16"), R("ADB"), 0.0, MUL, ADD)
+    ad = R("DGS", 15, 192, 16)
+    tt(w6(17), R("HW", 0, 6), R("DUM", 0, 6), SUB)
+    tt(w6(18), w6(8), R("DUM", 6, 12), SUB)
+    tt(w6(19), w6(12), R("DUM", 12, 18), SUB)
+    tt(w6(20, 12), w6(17, 12), ad, MUL)
+    tt(w6(22), w6(19), R("DGS", 15, 96, 16), MUL)
+    tt(w6(20, 18), w6(20, 18), R("DUM"), ADD)
+    hl, hyl, sl = R("LU3", 0, 6), R("LU3", 0, 12), R("LU3", 12, 18)
+    cp(R("LU3", 0, 18), w6(20, 18))
+    gat(R("XS"), R("XW", 0, W), R("LU", 52, 58), "s")
+    tt(R("XI", 0, 96), R("XS"), R("XL"), ADD)
+    ts(R("XI", 96, 192), R("XI", 0, 96), 1, None, AluOpType.arith_shift_right)
+    gat(R("FS"), R("FGW", 0, W), R("LU", 52, 58), "s")
+    ts(R("FM"), R("SEV"), R("COL", 6, 7), R("COL", 7, 8), MUL, ADD)
+    tt(R("FDL"), R("HREP"), R("FS"), SUB)
+    tt(R("FDL"), R("FDL"), R("FM"), MUL)
+    tt(R("FDL"), R("FDL"), R("FS"), ADD)
+    if t < 3:
+        ts(R("NHF"), sr, -3269.0, R("COL", 6, 7), ADD, MUL)
+        ts(R("NHY", 0, 96), R("NHF"), 3264.0, None, ADD)
+        ts(R("SLM"), ar, R("COL", 12, 13), None, EQ)
+        ts(R("GY"), R("SY"), -1.0, 3264.0, MUL, ADD)
+        tt(R("GY"), R("GY"), R("SLM"), MUL)
+        tt(R("NHY", 96, 192), R("GY"), R("SY"), ADD)
+        scat(R("BAD"), hl, R("O1B", 0, 96))
+        scat(R("SNW"), hyl, R("NHY"))
+    scat(R("FGW"), sl, R("FDL"))
+    scat(R("XW"), sl, R("XI", 96, 192))
+
+
+_d("LU3", 24, "uint16")
+
+
+def send(t):
+    fn, mb = "FNW%d" % t, "MB%d" % t
+    tt(R("LS6", 0, 6), w6(7), w6(10), SUB)
+    tot, pre = R("P4", 480, 486), R("P4", 488, 494)
+    mm([(tot, R("ONEB"), R("LS6", 0, 6))])
+    mm([(pre, R("TRIN"), R("LS6", 0, 6))])
+    scan(R("RW2", 0, 6), R("O1F", 0, 6), tot, 0.0, MUL, ADD)
+    tt(R("RW2", 6, 12), R("RW2", 0, 6), pre, ADD)
+    ts(R("RW2", 12, 18), R("RW2", 6, 12), 32.5, None, LT)
+    tt(R("RW2", 12, 18), R("RW2", 12, 18), R("LS6", 0, 6), MUL)
+    tt(R("RW2", 18, 24), R("RW2", 6, 12), R("DS1", 0, 6), SUB)
+    tt(R("RW2", 18, 24), R("RW2", 18, 24), R("RW2", 12, 18), MUL)
+    tt(R("RW2", 18, 24), R("RW2", 18, 24), R("DS1", 0, 6), ADD)
+    ts(R("LUS", 0, 6), R("RW2", 18, 24), -1.0, None, ADD)
+    ts(R("FN1"), R("FH"), 1.0, R("COL", 8, 9), ADD, MUL)
+    act(R("FN2"), R("HREP"), AF.Copy, scale=R("COL", 10, 11))
+    tt(R("FN1"), R("FN1"), R("FN2"), ADD)
+    scat(R(fn), R("LUS", 0, 6), R("FN1"))
+    scat(R(mb, 32, 160), R("LUS", 0, 6), R("XL"))
+    ts(R(mb, 0, 32), R(fn, 0, 32), R("COL", 8, 9), None, MUL)
+    op("g", ("send", t), [R(mb, 0, 64)], [], 0.6, 1.0, "ls", NENG)
+
+
+_d("RW2", 24)
+_d("LUS", 8, "uint16")
+
+
+def comeback(t):
+    rr, fn = "RR%d" % t, "FNW%d" % (t - 1)
+    op("n", None, [R("RB%d" % t)], [R(rr)], 0.0, 3.0, "rr%d" % t, NENG)
+    a = 3280 + 32 * (t - 1)
+    if t < 3:
+        mm([(R("P2", 374, 406), R("SEL0"), R(fn, 0, 32))])
+        tt(R("HPD"), R("P2", 374, 406), R("DUMR"), SUB)
+        tt(R("HPD"), R("HPD"), R("MASK", 0, 32), MUL)
+    ts(R("FL"), R(rr), 1000.0, None, LT)
+    if t < 3:
+        tt(R("FLN"), R("FL"), R("HPD"), MUL)
+        scan(R("DGS", 448, 480), R("RS16", 0, 32), R("FLN"), 0.0, MUL, ADD)
+        tt(R("RW", 30, 32), R("DGS", 448 + 15, 480, 16), R("DUMW", 0, 2), ADD)
+        cp(R("LU", 44, 46), R("RW", 30, 32))
+        scat(R("BAD"), R("LU", 44, 46), R("O1B", 0, 32))
+        ts(R("BAD", a, a + 32), R(rr), 1000.0, None, GE)
+        gat(R("CUR"), R("SNW"), R("LU", 44, 46))
+        tt(R("FLN"), R("FL"), R("NC", 32 * t - 32, 32 * t), MUL)
+        tt(R("CUR2"), R("CUR"), R("FLN"), ADD)
+        scat(R("SNW"), R("LU", 44, 46), R("CUR2"))
+    tt(R("XW", a, a + 32), R(rr), R("FL"), MUL)
+    tt(R("FGW", a, a + 32), R(fn, 0, 32), R("FL"), MUL)
+
+
+def store():
+    fill(R("XW", M, M + 16), 0.0)
+    dma("y", "o1", None, R("XW", 0, W), oap=lambda T: T.xo[:, :], us=6.0)
+    dma("a", "o2", None, R("FGW", 0, W, p0=0, ps=16), oap=lambda T: T.fo[:, :], us=4.0)
+    dma("y", "o3", None, R("FGW", 0, W, p0=1, ps=16), oap=lambda T: T.f2o[:, :], us=4.0)
+
+
+def schedule():
+    load()
+    consts()
+    load2()
+    for t in range(NT):
+        if t:
+            arrivals(t)
+        lanes(t)
+        own(t)
+        if t:
+            comeback(t)
+    store()
+    last = {}
+    for o in OPS:
+        dep = set()
+        qq = "s" if o["q"] == "a" else o["q"]
+        for kind, lst in (("r", o["rd"]), ("w", o["wr"])):
+            for r in lst:
+                ps = is_ps(r)
+                for (k2, r2, j) in last.get(r[0], []):
+                    if ps:
+                        if OPS[j]["q"] != o["q"] or ((kind == "w" or k2 == "w") and hit(r, r2)):
+                            dep.add(j)
+                    elif (kind == "w" or k2 == "w") and hit(r, r2):
+                        dep.add(j)
+        o["dep"] = sorted(dep)
+        for kind, lst in (("r", o["rd"]), ("w", o["wr"])):
+            for r in lst:
+                h = last.setdefault(r[0], [])
+                if kind == "w" and not is_ps(r):
+                    h[:] = [e for e in h if not (r[3] == 1 and r[6] == 1 and e[1][1] >= r[1] and e[1][2] <= r[2] and e[1][4] >= r[4] and e[1][5] <= r[5])]
+                h.append((kind, r, o["i"]))
+    n = len(OPS)
+    succ = [[] for _ in range(n)]
+    for o in OPS:
+        for j in o["dep"]:
+            succ[j].append(o["i"])
+    rank = [0.0] * n
+    for i in range(n - 1, -1, -1):
+        o = OPS[i]
+        rank[i] = o["cost"] + o["tail"] + max([rank[j] + WAKE for j in succ[i]], default=0.0)
+    left = [len(o["dep"]) for o in OPS]
+    ready = {i: 0.0 for i in range(n) if not left[i]}
+    free, end, order = {}, [0.0] * n, []
+    while ready:
+        best = None
+        for i, rt in ready.items():
+            q = "s" if OPS[i]["q"] == "a" else OPS[i]["q"]
+            st = max(rt, free.get(q, 0.0)) if q != "n" else rt
+            key = (st, -rank[i], i)
+            if best is None or key < best[0]:
+                best = (key, i, q, st)
+        _, i, q, st = best
+        if q != "n" and OPT["slack"]:
+            lim, top = st + OPT["slack"], rank[i]
+            for j, rt in ready.items():
+                if ("s" if OPS[j]["q"] == "a" else OPS[j]["q"]) == q and rank[j] > top + OPT["slack"] and max(rt, free.get(q, 0.0)) <= lim:
+                    i, top, st = j, rank[j], max(rt, free.get(q, 0.0))
+        del ready[i]
+        o = OPS[i]
+        if q != "n":
+            free[q] = st + o["cost"]
+        end[i] = st + o["cost"] + o["tail"]
+        order.append(i)
+        for j in succ[i]:
+            left[j] -= 1
+            if not left[j]:
+                ready[j] = max(end[d] + (WAKE if OPS[d]["q"] != "n" else 0.0) for d in OPS[j]["dep"])
+    return order, max(end)
+
+
+PLAN = {}
+QSEM = {"v": "sv", "s": "ss", "t": "st", "g": "sg"}
+
+
+def rank_program(g, core, T, topo):
+    rank = T.rank_of(core)
+    if rank is None:
+        return
+    if not PLAN:
+        PLAN["order"], PLAN["est"] = schedule()
+    eng = {"v": g.vector, "s": g.scalar, "a": g.scalar, "t": g.tensor, "g": g, "y": g.sync}
+    done, total, seen = {}, {}, {q: {} for q in "vstgy"}
+
+    def remote(dst, out, src, sem):
+        rid, pid, _ = topo.addr(dst)
+        m = 0
+        for e in topo.engines(core, dst)[:NENG]:
+            m |= 1 << e
+        g.remote_dma(out_ap=out, in_ap=src, remote_sem=T.sem[sem], local_sem=T.sem.ls, pid=pid, routing_id=rid, dma_engine_mask=m)
+
+    for i in PLAN["order"]:
+        o = OPS[i]
+        if o["q"] == "n":
+            total[o["sem"]] = o["n"]
+            done[i] = (o["sem"], o["n"])
+            continue
+        q = "s" if o["q"] == "a" else o["q"]
+        need = {}
+        for j in o["dep"]:
+            if OPS[j]["sem"] == "ls":
+                continue
+            s, v = done[j]
+            need[s] = max(need.get(s, 0), v)
+        for s in sorted(need):
+            if seen[q].get(s, 0) < need[s]:
+                eng[o["q"]].wait_ge(T.sem[s], need[s])
+                seen[q][s] = need[s]
+        fn = o["fn"]
+        if isinstance(fn, tuple):
+            what, t = fn
+            if what == "send":
+                remote(T.cores[(rank + 1 + t) % 8], T["AR%d" % (t + 1)][:, :], T["MB%d" % t][:, 0:64], "ar%d" % (t + 1))
+            else:
+                remote(T.cores[(rank - t) % 8], T["RR%d" % t][:, :], T["RB%d" % t][:, :], "rr%d" % t)
+            total["ls"] = total.get("ls", 0) + NENG
+            done[i] = ("ls", total["ls"])
+            continue
+        r = fn(g, T)
+        s = o["sem"] or QSEM[o["q"]]
+        for x in (r if isinstance(r, list) else [r]):
+            x.then_inc(T.sem[s], o["n"])
+            total[s] = total.get(s, 0) + o["n"]
+        done[i] = (s, total[s])
+    for s in sorted(total):
+        if seen["g"].get(s, 0) < total[s]:
+            g.wait_ge(T.sem[s], total[s])

@@ -10,9 +10,9 @@ SEG = 17
 NSEG = 8 * SEG
 BIGX = 4096.0
 NENG = 8
-CH = {"A": (("s", 24), ("v", 40), ("v", 32)), "B": (("s", 24), ("v", 40), ("v", 32)), "R": (("s", 16), ("v", 16))}
-AV = {"A": 6, "B": 2, "R": 0}
-NR = {"A": "s", "B": "v", "R": "s"}
+CH = {"A": (("s", 32), ("v", 32), ("v", 32)), "B": (("s", 24), ("v", 40), ("v", 32)), "R": (("s", 8), ("v", 24))}
+AV = {"A": 2, "B": 4, "R": 4}
+NR = {"A": "s", "B": "s", "R": "v"}
 GQ = [4]
 OPT = {"slack": 0.0, "pe": 0.0006, "bias": {}}
 WAKE = 0.12
@@ -32,11 +32,11 @@ def _d(name, cols, dtype="float32", where="sbuf", rows=128):
         SCRATCH[name] = (where, [rows, cols], dtype)
 
 
-for _n, _c, _t in (("SNW", SNWW, "int32"), ("XW", XWW, "bfloat16"), ("FGW", FGWW, "float32"), ("BAD", BADW, "bfloat16"),
+for _n, _c, _t in (("SNW", SNWW, "int32"), ("XW", XWW, "bfloat16"), ("FGW", FGWW, "float32"), ("F1R", FGWW, "float32"), ("F2R", FGWW, "float32"), ("HPR", 32, "float32"), ("BAD", BADW, "bfloat16"),
                    ("GD", 204, "int32"), ("FD", 204, "int32"), ("GDB", 204, "bfloat16"), ("GDF", 204, "float32"), ("FDF", 204, "float32"),
                    ("GB8", M, "bfloat16"), ("WC", 1, "bfloat16"), ("NGB", 212, "float32"),
                    ("OKR", 212, "bfloat16"), ("CUM", NB, "float32"), ("SJ", 6 * NB, "bfloat16"), ("HR", 8, "float32"), ("RHO", 8, "uint16"),
-                   ("RK", 212, "float32"), ("RG", 96, "float32"), ("VG", 96, "float32"), ("HV", 96, "float32"),
+                   ("RK", 212, "float32"), ("VG", 96, "bfloat16"),
                    ("HREP", 96, "float32"), ("PREP", 96, "float32"), ("FH", 96, "float32"), ("FP", 96, "float32"),
                    ("XL", 96, "bfloat16"), ("XLE", 1536, "bfloat16"), ("XLR", 512, "bfloat16"),
                    ("DGM", 3 * 192, "float32"), ("DGS", 3 * 192, "float32"), ("HW", 8, "float32"), ("PWF", 8, "float32"),
@@ -45,9 +45,10 @@ for _n, _c, _t in (("SNW", SNWW, "int32"), ("XW", XWW, "bfloat16"), ("FGW", FGWW
                    ("J", NSEG, "float32"), ("T1", 144, "float32"), ("T2", 144, "float32"),
                    ("ONEF", 128, "float32"), ("ONEB", 128, "bfloat16"), ("BLK", 8, "bfloat16"), ("TRIN", 128, "bfloat16"), ("ZW", 144, "bfloat16"), ("Z8", 144, "bfloat16"),
                    ("SEL0", 128, "float32"), ("SEL1", 128, "float32"), ("SEL2", 128, "bfloat16"), ("MASK", 192, "float32"), ("BL", 8, "float32"), ("IDF", 128, "float32"),
-                   ("PERF", NSEG, "float32"), ("PERB", NSEG, "bfloat16"), ("CK", NSEG, "bfloat16"), ("CP1", NSEG, "float32"), ("CP2", NSEG, "float32"),
+                   ("PERF", NSEG, "float32"), ("PERB", NSEG, "bfloat16"), ("CK", NSEG, "bfloat16"), ("CP1", NSEG, "bfloat16"), ("CP2", NSEG, "bfloat16"),
                    ("O1B", 128, "bfloat16"), ("O1F", 216, "float32"), ("RST", NSEG, "float32"), ("KB", 8, "float32"), ("KROW", 96, "float32"),
-                   ("VAL0", 216, "float32"), ("VAL1", 216, "float32"), ("VAL2", 216, "float32"), ("VAL3", 216, "float32"),
+                   ("VAL0", 216, "bfloat16"), ("VAL1", 216, "bfloat16"), ("VAL2", 216, "bfloat16"), ("VAL3", 216, "bfloat16"), ("TRIB", 16, "bfloat16"),
+                   ("TRI2", 128, "bfloat16"), ("ONEL", 128, "bfloat16"), ("OH", 96, "bfloat16"),
                    ("LW", 8, "float32"), ("DUM", 18, "float32"), ("DS1", 8, "float32"), ("DUMR", 32, "float32"), ("DUMW", 8, "float32"), ("RS16", 192, "float32"), ("TRIM", 96, "float32"),
                    ("NC", 96, "float32"), ("WB", 128, "bfloat16"), ("BLQ", 8, "float32"), ("IDB", 128, "bfloat16"), ("IDN", 128, "bfloat16"), ("O64", 128, "float32"), ("RSM", NSEG, "float32"),
                    ("W6", 192, "float32"), ("I6", 24, "int32"), ("EXY", 96, "float32"), ("EXS", 96, "float32"), ("EXA", 96, "bfloat16"),
@@ -111,10 +112,12 @@ def is_ps(r):
 
 CY = 0.00083
 OPS = []
+CLS = ["I"]
+BON = {"I": 0.0, "L": 0.0, "A": 0.0, "B": 0.0, "R": 0.0, "S": 0.0, "T": 0.0, "C": 0.0}
 
 
 def op(q, fn, rd, wr, cost, tail=0.0, sem=None, n=1, count=1):
-    OPS.append({"q": q, "fn": fn, "rd": [r for r in rd if r], "wr": wr, "cost": cost, "tail": tail, "sem": sem, "n": n, "count": count, "i": len(OPS)})
+    OPS.append({"c": CLS[0], "q": q, "fn": fn, "rd": [r for r in rd if r], "wr": wr, "cost": cost, "tail": tail, "sem": sem, "n": n, "count": count, "i": len(OPS)})
 
 
 def two(*rs):
@@ -137,7 +140,11 @@ def gat(out, win, off, q="v"):
 
 
 def gsub(out, win, off, b):
-    op("v", lambda g, T: g.vector.tensor_tensor(ap(T, out), ap(T, win).indirect(ap(T, off)), ap(T, b), SUB), [win, off, b], [out], 0.05 + wid(out) * 1.56 * CY)
+    gop(out, win, off, b, SUB)
+
+
+def gop(out, win, off, b, o):
+    op("v", lambda g, T: g.vector.tensor_tensor(ap(T, out), ap(T, win).indirect(ap(T, off)), ap(T, b), o), [win, off, b], [out], 0.05 + wid(out) * 1.56 * CY)
 
 
 def scat(win, off, a):
@@ -267,23 +274,27 @@ def consts():
     fill(R("O1F"), 1.0)
     ts(R("LW", 0, 6), R("C128", 0, 6), 16.0, PLO, MUL, ADD)
     ts(R("KB", 0, 6), R("LW", 0, 6), 0.5, None, ADD)
-    ts(R("KROW"), R("C128", 0, 96), 1.0, None, ADD)
+    ts(R("KROW"), R("C128", 0, 96), 4097.0, None, ADD)
     for k in range(3):
         ts(R("DUM", 6 * k, 6 * k + 6), R("LW", 0, 6), float(W + (96 if k == 1 else 0)), None, ADD)
     ts(R("DS1", 0, 6), R("LW", 0, 6), 33.0, None, ADD)
     ts(R("DUMR"), R("C128", 0, 32), float(W + 192), None, ADD)
     ts(R("DUMW", 0, 2), R("LW", 0, 2), float(W + 192), None, ADD)
     ts(R("RS16"), R("CLO"), 0.5, None, GT)
-    ts(R("TRIM"), R("CLO", 0, 96), PLO, 20000.0, LE, MUL)
+    ts(R("TRIB"), R("CLO", 0, 16), PLO, 20000.0, LE, MUL)
+    ts(R("T2", 0, 128), R("IDF"), 4096.0, None, MUL)
+    tt(R("TRI2"), R("T2", 0, 128), R("TRIN"), ADD)
+    ts(R("ONEL"), R("ONEF"), PLO, None, MUL)
+    ts(R("COL", 13, 14), R("COL", 6, 7), -1.0, None, MUL)
+    ts(R("COL", 14, 15), R("COL", 7, 8), -1.0, 1.0, MUL, ADD)
     for t in range(1, 4):
         ts(R("NC", 32 * t - 32, 32 * t), R("C128", 0, 32), float(16 + 32 * (t - 1)), R("COL", 6 + t, 7 + t), ADD, MUL)
     for t in range(4):
         s = 66 * t
-        iota(R("VAL%d" % t, 0, NB - s), [[16, NB - s]], 16 * s - M, 0)
+        iota(R("VAL%d" % t, 0, NB - s), [[16, NB - s]], 16 * s, 0)
         if s:
-            iota(R("VAL%d" % t, NB - s, NB), [[16, s]], -M, 0)
-        iota(R("VAL%d" % t, NB, 216), [[0, 216 - NB]], 0, 0)
-        ts(R("VAL%d" % t), R("VAL%d" % t), PLO, None, ADD)
+            iota(R("VAL%d" % t, NB - s, NB), [[16, s]], 0, 0)
+        iota(R("VAL%d" % t, NB, 216), [[0, 216 - NB]], M, 0)
     fill(R("P2", 0, 2 * NSEG), 0.0)
     fill(R("RK", NB, 212), 0.0)
     fill(R("OKR", NB, 212), 0.0)
@@ -310,8 +321,10 @@ def load():
     dma("a", "ff1", wh("DFF"), R("FDF"))
     dma("a", "gf1", wh("DGF"), R("GDF"))
     dma("a", "gb2", R("GB8", p1=8), wh("DGB"))
-    dma("a", "ff2", R("FGW", 0, M, p0=0, ps=16), wh("DFF"))
-    dma("a", "ff3", R("FGW", 0, M, p0=1, ps=16), wh("DFF"))
+    fill(R("F1R", M, FGWW), 0.0)
+    fill(R("F2R", M, FGWW), 0.0)
+    for k in (1, 2):
+        op("y", lambda g, T, k=k: [g.sync.dma_start(T["F%dR" % k][i:128:16, 0:M], T.DFF[:, :]) for i in range(16)], [wh("DFF")], [R("F%dR" % k, 0, M)], 1.6, 5.0, "d_ff%d" % (k + 1), 16)
     dma("a", "gf2", R("FGW", 0, M, p0=2, ps=16), wh("DGF"))
     fill(R("SNW", M, SNWW), 3264)
     fill(R("XW", M, M + 16), BIGX)
@@ -336,13 +349,14 @@ def diag(src, n, k, msk=True):
 
 
 def level(ch, bank, nl, off, bar, xle, last):
+    CLS[0] = ch
     kc = nl // 16
     sf, su, dd = R("SF" + ch), R("SU" + ch), "DD" + ch
-    gat(sf, R("SNW", 0, W), off)
-    cp(su, sf)
+    gat(su, R("SNW", 0, W), off)
+    cp(sf, su)
     cpr = R("CP2" if last else "CP1", p1=1)
     pt, pk, pw = R(bank, 0, NSEG, p1=nl), R(bank, NSEG, 2 * NSEG, p1=nl), R(bank, 300, 300 + kc)
-    mm([(pt, R("O1F", 0, nl, p1=1), cpr), (pt, sf, R("PERF"))])
+    mm([(pt, R("O1B", 0, nl, p1=1), cpr), (pt, sf, R("PERF"))])
     keys = [(pk, R("O1B", 0, nl, p1=1), R("CK", p1=1))]
     if bar:
         tt(R("EQ" + ch), sf, bar, EQ)
@@ -396,13 +410,13 @@ def argmin(ch, pk, pt, np_, ns, last=False):
 
 def guest_level(off):
     sf, su, dd = R("SFR"), R("SUR"), "DDR"
-    gat(sf, R("SNW", 0, W), off)
-    cp(su, sf)
+    gat(su, R("SNW", 0, W), off)
+    cp(sf, su)
     differences("R", dd, "XLR")
     n = GQ[0]
     qs = [(q, {"p0": 16 * n * q, "p1": 16 * n * q + 32}) for q in range(8 // n)]
     k = n * SEG
-    mms([[(R("P2", 0, k, **p), R("O1F", 0, 32, p1=1), R("CP1", 0, k, p1=1)), (R("P2", 0, k, **p), sf, R("PERF", k * q, k * q + k))] for q, p in qs])
+    mms([[(R("P2", 0, k, **p), R("O1B", 0, 32, p1=1), R("CP1", 0, k, p1=1)), (R("P2", 0, k, **p), sf, R("PERF", k * q, k * q + k))] for q, p in qs])
     mms([[(R("P2", k, 2 * k, **p), R("O1B", 0, 32, p1=1), R("CK", 0, k, p1=1))]
          + [(R("P2", k + 1 + s, 2 * k, SEG, **p), R(dd, s, 512, 16), R("BLK", n * q, n * q + n)) for s in range(16)] for q, p in qs])
     argmin("R", R("P2", k, 2 * k), R("P2", 0, k), 128, n)
@@ -449,37 +463,36 @@ def lanes(t):
         tt(R("OKR", NB - s, NB), R("P3", 0, s), R("NGB", 0, s), EQ)
     tot, pre = R("P3", 256, 256 + NB), R("P3", 0, NB)
     mm([(tot, R("ONEB"), R("OKR", 0, NB))])
-    mm([(pre, R("TRIN"), R("OKR", 0, NB))])
+    mm([(pre, R("TRI2"), R("OKR", 0, NB))])
     scan(R("CUM"), R("O1F", 0, NB), tot, 0.0, MUL, ADD)
     for k in range(6):
         act(R("SJ", NB * k, NB * k + NB), R("CUM"), AF.Sign, scale=-1.0, bias=R("KB", k, k + 1), acc=R("HR", k, k + 1))
     tt(R("RK", 0, NB), R("CUM"), pre, ADD)
-    tt(R("RK", 0, NB), R("RK", 0, NB), R("OKR", 0, NB), MUL)
     ts(R("RHO", 0, 6), R("HR", 0, 6), 0.5, NB / 2, MUL, ADD)
     gat(R("VG"), R("VAL%d" % t, 0, 212), R("RHO", 0, 6), "s")
-    gat(R("RG"), R("RK"), R("RHO", 0, 6))
-    tt(R("RG"), R("RG"), R("KROW"), EQ)
-    tt(R("HV"), R("RG"), R("VG"), MUL)
-    mm([(R("P4", 0, 96), R("O64", p1=1), R("O1F", 0, 96, p1=1)), (R("P4", 0, 96), R("ONEF"), R("HV"))])
+    gop(R("OH"), R("RK"), R("RHO", 0, 6), R("KROW"), EQ)
+    mm([(R("P4", 0, 96), R("IDB"), R("VG")), (R("P4", 0, 96), R("ONEL"), R("OH"))])
     hs = diag(R("P4", 0, 96), 96, 0)
     cp(R("LU", 0, 6), hs)
     act(R("HREP"), R("P4", 0, 96))
     act(R("HW", 0, 6), hs)
-    gat(R("FH"), R("FGW", 0, W), R("LU", 0, 6))
+    ft = "F%dR" % (1 + t % 2)
+    gop(R("DGM", 192, 288), R(ft, 0, W), R("LU", 0, 6), R("MASK", 0, 96), MUL)
+    scan(R("DGS", 192, 288), R("RS16", 0, 96), R("DGM", 192, 288), 0.0, MUL, ADD)
+    ps = R("DGS", 192 + 15, 288, 16)
+    cp(R("LU", 6, 12), ps)
+    act(R("PWF", 0, 6), ps)
+    gat(R("PREP"), R(ft, 0, W), R("LU", 0, 6), "s")
+    gop(R("DGM", 0, 96), R(ft, 0, W), R("LU", 6, 12), R("MASK", 0, 96), MUL)
+    scan(R("DGS", 0, 96), R("RS16", 0, 96), R("DGM", 0, 96), 0.0, MUL, ADD)
+    cp(R("LU", 12, 18), R("DGS", 15, 96, 16))
+    gat(R("FH"), R("FGW", 0, W), R("LU", 0, 6), "s")
     gat(R("XL"), R("XW", 0, W), R("LU", 0, 6))
     for k in range(16):
         if k % 2:
             act(R("XLE", k, 1536, 16), R("XL"))
         else:
             cp(R("XLE", k, 1536, 16), R("XL"))
-    sel = R("SEL%d" % (t % 2))
-    mm([(R("P4", 96, 192), sel, R("FH"))])
-    ps = diag(R("P4", 96, 192), 96, 1)
-    cp(R("LU", 6, 12), ps)
-    act(R("PWF", 0, 6), ps)
-    gat(R("FP"), R("FGW", 0, W), R("LU", 6, 12))
-    mm([(R("P4", 192, 288), sel, R("FP"))])
-    cp(R("LU", 12, 18), diag(R("P4", 192, 288), 96, 0))
 
 
 def w6(k, n=6):
@@ -490,7 +503,7 @@ def own(t):
     pa = level("A", "P0", 96, R("LU", 6, 12), R("P4", 0, 96), "XLE", False)
     cp(R("LU", 18, 24), pa)
     act(w6(1), pa)
-    pb = level("B", "P1", 96, R("LU", 12, 18), R("P4", 96, 192), "XLE", False)
+    pb = level("B", "P1", 96, R("LU", 12, 18), R("PREP"), "XLE", False)
     cp(R("LU", 24, 30), pb)
     pa = level("A", "P0", 96, R("LU", 18, 24), None, "XLE", True)
     act(w6(0), pa)
@@ -498,6 +511,7 @@ def own(t):
     cp(R("LU", 46, 52), pb)
     act(w6(3), pb)
     pb = level("B", "P1", 96, R("LU", 46, 52), None, "XLE", True)
+    CLS[0] = "T"
     ts(w6(7), R("HW", 0, 6), 3264.0, None, NEQ)
     ts(w6(9), R("PWF", 0, 6), 64.0, None, GE)
     tt(w6(9), w6(9), w6(7), MUL)
@@ -510,7 +524,6 @@ def own(t):
     tt(w6(8), w6(5), w6(3), MUL)
     tt(w6(8), w6(8), w6(25), ADD)
     ts(w6(26), w6(8), 5.0, None, ADD)
-    ts(w6(25), w6(8), 10005.0, None, ADD)
     ts(w6(6), pb, 3264.0, None, NEQ)
     tt(w6(6), w6(6), w6(23), MUL)
     tt(w6(10), w6(6), w6(11), ADD)
@@ -521,46 +534,45 @@ def own(t):
     cp(R("LU", 52, 58), R("I6", 6, 12))
     cp(R("LU", 58, 64), w6(8))
     if t < 3:
+        CLS[0] = "S"
         send(t)
+        CLS[0] = "T"
     cp(w6(12, 12), R("I6", 6, 18))
     ts(w6(27), R("I6", 6, 12), 5.0, None, ADD)
-    ts(w6(14), w6(10), -10000.0, None, MUL)
-    tt(w6(14), w6(14), w6(25), ADD)
     tt(w6(15), w6(26), w6(10), MUL)
     tt(w6(16), w6(27), w6(10), MUL)
-    for b, k, q in (("EXY", 14, 0), ("EXS", 27, 1), ("EXA", 13, 1)):
+    for b, k, q in (("EXY", 26, 1), ("EXS", 27, 1), ("EXA", 13, 1)):
         for l in range(6):
             o, sc = R(b, 16 * l, 16 * l + 16), R("W6", 6 * k + l, 6 * k + l + 1)
             if q:
                 act(o, R("MASK", 0, 16), AF.Copy, scale=sc)
             else:
                 ts(o, R("MASK", 0, 16), sc, None, MUL)
-    yr, sr, ym, sm = [R("P6", 96 * k, 96 * k + 96) for k in range(4)]
-    mm([(yr, R("ONEF"), R("EXY"))])
-    mm([(sr, R("ONEF"), R("EXS"))])
-    mm([(ym, R("ONEF"), R("EXY")), (ym, R("IDF"), R("TRIM"))])
-    mm([(sm, R("ONEF"), R("EXS")), (sm, R("IDF"), R("TRIM"))])
-    ar = R("P4", 288, 384)
-    mm([(ar, R("ONEB"), R("EXA"))])
+    sr, ar, cfl = R("P4", 96, 192), R("P4", 288, 384), R("P4", 384, 480)
     cf = []
-    for v in range(2):
+    for v, b, bank in ((0, "EXY", "P6"), (1, "EXS", "P3")):
+        at, gr = 0, []
         for l in range(6):
-            sc = R("W6", 6 * (15 + v) + l, 6 * (15 + v) + l + 1)
-            b = 192 + 96 * v + 16 * l
-            ts(R("EQM", 96 * v + 16 * l, 96 * v + 16 * l + 16), R("P6", b, b + 16), sc, None, EQ)
-            if l < 5:
-                n, e = 80 - 16 * l, 480 * v + 96 * l
-                ts(R("EQP", e, e + n), R("P6", 96 * v + 16 * l + 16, 96 * v + 96), sc, None, EQ)
-                cf.append((R("P4", 384 + 16 * l + 16, 480), R("ONEB"), R("EQP", e, e + n)))
-    cfl = R("P4", 384, 480)
-    mm([(cfl, R("ONEB"), R("EQM", 0, 96))] + cf + [(cfl, R("ONEB"), R("EQM", 96, 192))])
+            n = 96 - 16 * l
+            gr.append([(R(bank, at, at + n), R("ONEF"), R(b, 16 * l, 96)), (R(bank, at, at + 16), R("IDB"), R("TRIB"))])
+            at += n
+        mms(gr)
+        at = 0
+        for l in range(6):
+            n = 96 - 16 * l
+            ts(R("EQP", 336 * v + at, 336 * v + at + n), R(bank, at, at + n), R("W6", 6 * (15 + v) + l, 6 * (15 + v) + l + 1), None, EQ)
+            cf.append((R("P4", 384 + 16 * l, 480), R("ONEB"), R("EQP", 336 * v + at, 336 * v + at + n)))
+            at += n
+    mm([(sr, R("ONEF"), R("EXS"))])
+    mm([(ar, R("ONEB"), R("EXA"))])
+    mm(cf)
     gat(R("SY"), R("SNW", 0, W), R("LU", 58, 64))
     ts(R("NEY"), R("SY"), 3264.0, None, NEQ)
     sv = R("P4", 192, 288)
     mm([(sv, R("ONEB"), R("NEY"))])
     ts(R("SEV"), sv, 1.5, None, GT)
-    ts(R("FR"), yr, 9000.0, None, LT)
-    tt(R("FR"), R("FR"), R("MASK", 0, 96), MUL)
+    for l in range(6):
+        act(R("FR", 16 * l, 16 * l + 16), R("MASK", 0, 16), AF.Copy, scale=R("W6", 60 + l, 61 + l))
     tt(R("ADB", 0, 96), cfl, R("FR"), LT)
     tt(R("ADB", 96, 192), R("ADB", 0, 96), R("SEV"), MUL)
     scan(R("DGS", 0, 192), R("RS16"), R("ADB"), 0.0, MUL, ADD)
@@ -574,13 +586,12 @@ def own(t):
     hl, hyl, sl = R("LU3", 0, 6), R("LU3", 0, 12), R("LU3", 12, 18)
     cp(R("LU3", 0, 18), w6(20, 18))
     gat(R("XS"), R("XW", 0, W), R("LU", 52, 58), "s")
-    tt(R("XI", 0, 96), R("XS"), R("XL"), ADD)
-    ts(R("XI", 96, 192), R("XI", 0, 96), 1, None, AluOpType.arith_shift_right)
-    gat(R("FS"), R("FGW", 0, W), R("LU", 52, 58), "s")
-    ts(R("FM"), R("SEV"), R("COL", 6, 7), R("COL", 7, 8), MUL, ADD)
-    tt(R("FDL"), R("HREP"), R("FS"), SUB)
-    tt(R("FDL"), R("FDL"), R("FM"), MUL)
-    tt(R("FDL"), R("FDL"), R("FS"), ADD)
+    px = R("P6", 336, 432)
+    mm([(px, R("IDB"), R("XS")), (px, R("IDB"), R("XL"))])
+    ts(R("XI", 96, 192), px, 0.5, -0.25, MUL, ADD)
+    tt(w6(30), w6(19), R("DGS", 96 + 15, 192, 16), MUL)
+    tt(w6(30), w6(30), R("DUM", 12, 18), ADD)
+    cp(R("LU3", 18, 24), w6(30))
     if t < 3:
         ts(R("NHF"), sr, -3269.0, R("COL", 6, 7), ADD, MUL)
         ts(R("NHY", 0, 96), R("NHF"), 3264.0, None, ADD)
@@ -590,7 +601,8 @@ def own(t):
         tt(R("NHY", 96, 192), R("GY"), R("SY"), ADD)
         scat(R("BAD"), hl, R("O1B", 0, 96))
         scat(R("SNW"), hyl, R("NHY"))
-    scat(R("FGW"), sl, R("FDL"))
+    scat(R("F2R"), sl, R("HREP"))
+    scat(R("F1R"), R("LU3", 18, 24), R("HREP"))
     scat(R("XW"), sl, R("XI", 96, 192))
 
 
@@ -628,8 +640,9 @@ def comeback(t):
     rr, fn = "RR%d" % t, "FNW%d" % (t - 1)
     op("n", None, [R("RB%d" % t)], [R(rr)], 0.0, 3.0, "rr%d" % t, NENG)
     a = 3280 + 32 * (t - 1)
+    mm([(R("P2", 374, 406), R("SEL0"), R(fn, 0, 32))])
+    act(R("HPR"), R("P2", 374, 406))
     if t < 3:
-        mm([(R("P2", 374, 406), R("SEL0"), R(fn, 0, 32))])
         tt(R("HPD"), R("P2", 374, 406), R("DUMR"), SUB)
         tt(R("HPD"), R("HPD"), R("MASK", 0, 32), MUL)
     ts(R("FL"), R(rr), 1000.0, None, LT)
@@ -645,14 +658,17 @@ def comeback(t):
         tt(R("CUR2"), R("CUR"), R("FLN"), ADD)
         scat(R("SNW"), R("LU", 44, 46), R("CUR2"))
     tt(R("XW", a, a + 32), R(rr), R("FL"), MUL)
-    tt(R("FGW", a, a + 32), R(fn, 0, 32), R("FL"), MUL)
+    tt(R("F1R", a, a + 32), R("HPR"), R("FL"), MUL)
+    tt(R("F2R", a, a + 32), R("HPR"), R("FL"), MUL)
+    if t < 3:
+        tt(R("FGW", a, a + 32), R(fn, 0, 32), R("FL"), MUL)
 
 
 def store():
     fill(R("XW", M, M + 16), 0.0)
     dma("y", "o1", None, R("XW", 0, W), oap=lambda T: T.xo[:, :], us=6.0)
-    dma("a", "o2", None, R("FGW", 0, W, p0=0, ps=16), oap=lambda T: T.fo[:, :], us=4.0)
-    dma("y", "o3", None, R("FGW", 0, W, p0=1, ps=16), oap=lambda T: T.f2o[:, :], us=4.0)
+    dma("a", "o2", None, R("F1R", 0, W, p0=0, ps=16), oap=lambda T: T.fo[:, :], us=4.0)
+    dma("y", "o3", None, R("F2R", 0, W, p0=0, ps=16), oap=lambda T: T.f2o[:, :], us=4.0)
 
 
 def schedule():
@@ -661,11 +677,15 @@ def schedule():
     load2()
     for t in range(NT):
         if t:
+            CLS[0] = "R"
             arrivals(t)
+        CLS[0] = "L"
         lanes(t)
         own(t)
         if t:
+            CLS[0] = "C"
             comeback(t)
+    CLS[0] = "I"
     store()
     last = {}
     for o in OPS:
@@ -696,6 +716,7 @@ def schedule():
     for i in range(n - 1, -1, -1):
         o = OPS[i]
         rank[i] = o["cost"] + o["tail"] + max([rank[j] + WAKE for j in succ[i]], default=0.0)
+    rank = [r + BON[o["c"]] for r, o in zip(rank, OPS)]
     left = [len(o["dep"]) for o in OPS]
     ready = {i: 0.0 for i in range(n) if not left[i]}
     free, end, order = {}, [0.0] * n, []

import numpy as np
from concourse.mybir import dt, AluOpType, AxisListType, ActivationFunctionType

M, L, S, NE, NT, W = 3264, 96, 32, 5, 4, 3376
NB = 211
XWW, FGWW = W + 96, W + 96
SNWW = W + 96 + 96 + 32
BADW = W + 96 + 96 + 32
SEG = 17
NSEG = 8 * SEG
BIGX = 4096.0
NENG = 8
CH = {"A": (("s", 32), ("v", 32), ("v", 32)), "B": (("s", 24), ("v", 40), ("v", 32)), "R": (("s", 8), ("v", 24))}
AV = {"A": 2, "B": 4, "R": 4}
NR = {"A": "s", "B": "s", "R": "v"}
GQ = [4]
OPT = {"slack": 0.0, "pe": 0.0006, "bias": {}}
WAKE = 0.12

SCRATCH, VS, PHYS = {}, {}, {}


def _d(name, cols, dtype="float32", where="sbuf", rows=128):
    VS[name] = (where, [rows, cols], dtype)
    if where == "sbuf" and cols < 2000 and not name[:2] in ("MB", "AR", "RB", "RR"):
        pool = "pool_" + dtype
        at = SCRATCH[pool][1][1] if pool in SCRATCH else 0
        PHYS[name] = (pool, at)
        SCRATCH[pool] = ("sbuf", [128, at + (cols + 15) // 16 * 16], dtype)
    else:
        PHYS[name] = (name, 0)
        SCRATCH[name] = (where, [rows, cols], dtype)


for _n, _c, _t in (("SNW", SNWW, "int32"), ("XW", XWW, "bfloat16"), ("FGW", FGWW, "float32"), ("F1R", FGWW, "float32"), ("F2R", FGWW, "float32"), ("HPR", 32, "float32"), ("BAD", BADW, "bfloat16"),
                   ("GD", 204, "int32"), ("FD", 204, "int32"), ("GDB", 204, "bfloat16"), ("GDF", 204, "float32"), ("FDF", 204, "float32"),
                   ("GB8", M, "bfloat16"), ("WC", 1, "bfloat16"), ("NGB", 212, "float32"),
                   ("OKR", 212, "bfloat16"), ("CUM", NB, "float32"), ("SJ", 6 * NB, "bfloat16"), ("HR", 8, "float32"), ("RHO", 8, "uint16"),
                   ("RK", 212, "float32"), ("VG", 96, "bfloat16"),
                   ("HREP", 96, "float32"), ("PREP", 96, "float32"), ("FH", 96, "float32"), ("FP", 96, "float32"),
                   ("XL", 96, "bfloat16"), ("XLE", 1536, "bfloat16"), ("XLR", 512, "bfloat16"),
                   ("DGM", 3 * 192, "float32"), ("DGS", 3 * 192, "float32"), ("HW", 8, "float32"), ("PWF", 8, "float32"),
                   ("LU", 64, "uint16"),
                   ("IT", 8, "int32"), ("COL", 16, "float32"), ("CI", 192, "int32"), ("CJ", 192, "int32"), ("C128", 192, "float32"), ("CHI", 144, "float32"), ("CLO", 192, "float32"),
                   ("J", NSEG, "float32"), ("T1", 144, "float32"), ("T2", 144, "float32"),
                   ("ONEF", 128, "float32"), ("ONEB", 128, "bfloat16"), ("BLK", 8, "bfloat16"), ("TRIN", 128, "bfloat16"), ("ZW", 144, "bfloat16"), ("Z8", 144, "bfloat16"),
                   ("SEL0", 128, "float32"), ("SEL1", 128, "float32"), ("SEL2", 128, "bfloat16"), ("MASK", 192, "float32"), ("BL", 8, "float32"), ("IDF", 128, "float32"),
                   ("PERF", NSEG, "float32"), ("PERB", NSEG, "bfloat16"), ("CK", NSEG, "bfloat16"), ("CP1", NSEG, "bfloat16"), ("CP2", NSEG, "bfloat16"),
                   ("O1B", 128, "bfloat16"), ("O1F", 216, "float32"), ("RST", NSEG, "float32"), ("KB", 8, "float32"), ("KROW", 96, "float32"),
                   ("VAL0", 216, "bfloat16"), ("VAL1", 216, "bfloat16"), ("VAL2", 216, "bfloat16"), ("VAL3", 216, "bfloat16"), ("TRIB", 16, "bfloat16"),
                   ("TRI2", 128, "bfloat16"), ("ONEL", 128, "bfloat16"), ("OH", 96, "bfloat16"),
                   ("LW", 8, "float32"), ("DUM", 18, "float32"), ("DS1", 8, "float32"), ("DUMR", 32, "float32"), ("DUMW", 8, "float32"), ("RS16", 192, "float32"), ("TRIM", 96, "float32"),
                   ("NC", 96, "float32"), ("WB", 128, "bfloat16"), ("BLQ", 8, "float32"), ("IDB", 128, "bfloat16"), ("IDN", 128, "bfloat16"), ("O64", 128, "float32"), ("RSM", NSEG, "float32"),
                   ("W6", 192, "float32"), ("I6", 24, "int32"), ("EXY", 96, "float32"), ("EXS", 96, "float32"), ("EXA", 96, "bfloat16"),
                   ("EQP", 960, "bfloat16"), ("EQM", 192, "bfloat16"), ("FR", 96, "float32"), ("ADB", 192, "float32"), ("SY", 96, "float32"), ("NEY", 96, "bfloat16"), ("SEV", 96, "float32"),
                   ("XS", 96, "bfloat16"), ("XI", 192, "int32"), ("FS", 96, "float32"), ("FM", 96, "float32"), ("FDL", 96, "float32"),
                   ("NHF", 96, "float32"), ("NHY", 192, "int32"), ("SLM", 96, "float32"), ("GY", 96, "float32"), ("LS6", 8, "bfloat16"), ("FN1", 96, "float32"), ("FN2", 96, "float32"),
                   ("RI", 32, "int32"), ("RI2", 32, "int32"), ("RW", 32, "float32"), ("FL", 32, "float32"), ("HPD", 32, "float32"), ("CUR", 32, "float32"), ("CUR2", 32, "int32"), ("FLN", 32, "float32")):
    _d(_n, _c, _t)
for _t in range(3):
    _d("MB%d" % _t, 160, "bfloat16")
    _d("FNW%d" % _t, 128, "float32")
    _d("AR%d" % (_t + 1), 64, "bfloat16")
    _d("RB%d" % (_t + 1), 32, "bfloat16")
    _d("RR%d" % (_t + 1), 32, "bfloat16")
for _c, _n in (("A", 96), ("B", 96), ("R", 32)):
    _d("SF" + _c, _n), _d("SU" + _c, _n, "uint16"), _d("DD" + _c, 16 * _n, "bfloat16"), _d("EQ" + _c, _n, "bfloat16")
    _d("WK" + _c, 5 * NSEG), _d("AA" + _c, 128)
for _t in range(8):
    _d("P%d" % _t, 512, "float32", "psum")
_d("DGB", M, "bfloat16", "dram", 8)
_d("DGF", M, "float32", "dram", 8)
_d("DFF", M, "float32", "dram", 8)

_DMAS = ["sn0", "sn1", "sn2", "sn3", "xin", "gin", "fin", "win", "gb1", "gb2", "ff1", "ff2", "ff3", "gf1", "gf2", "o1", "o2", "o3"]
SEMAPHORES = ["sv", "ss", "st", "sg", "ls"] + ["d_" + n for n in _DMAS] + ["ar%d" % t for t in (1, 2, 3)] + ["rr%d" % t for t in (1, 2, 3)]

ADD, SUB, MUL, MAX, MIN = AluOpType.add, AluOpType.subtract, AluOpType.mult, AluOpType.max, AluOpType.min
EQ, NEQ, LT, GE, GT, LE = AluOpType.is_equal, AluOpType.not_equal, AluOpType.is_lt, AluOpType.is_ge, AluOpType.is_gt, AluOpType.is_le
AF = ActivationFunctionType


def R(buf, a=0, b=None, step=1, p0=0, p1=None, ps=1):
    rows, cols = VS[buf][1]
    return (buf, a, cols if b is None else b, step, p0, rows if p1 is None else p1, ps)


def ap(T, r):
    n, o = PHYS[r[0]]
    if r[3] == 1 and r[6] == 1:
        return T[n][r[4]:r[5], o + r[1]:o + r[2]]
    return T[n][r[4]:r[5]:r[6], o + r[1]:o + r[2]:r[3]]


def wid(r):
    return (r[2] - r[1] + r[3] - 1) // r[3]


def _hit1(a0, a1, s, b0, b1, u):
    if a1 <= b0 or b1 <= a0:
        return False
    return not (s == u and s > 1 and (a0 - b0) % s)


def hit(x, y):
    return x[0] == y[0] and _hit1(x[1], x[2], x[3], y[1], y[2], y[3]) and _hit1(x[4], x[5], x[6], y[4], y[5], y[6])


def is_ps(r):
    return VS[r[0]][0] == "psum"


CY = 0.00083
OPS = []
CLS = ["I"]
BON = {"I": 0.0, "L": 0.0, "A": 0.0, "B": 0.0, "R": 0.0, "S": 0.0, "T": 0.0, "C": 0.0}


def op(q, fn, rd, wr, cost, tail=0.0, sem=None, n=1, count=1):
    OPS.append({"c": CLS[0], "q": q, "fn": fn, "rd": [r for r in rd if r], "wr": wr, "cost": cost, "tail": tail, "sem": sem, "n": n, "count": count, "i": len(OPS)})


def two(*rs):
    return all(VS[r[0]][2] in ("bfloat16", "uint16") for r in rs)


def _isr(s):
    return s if isinstance(s, tuple) else None


def cp(out, a):
    op("v", lambda g, T: g.vector.tensor_copy(ap(T, out), ap(T, a)), [a], [out], max(64, wid(a) * (0.5 if two(out, a) else 1)) * CY)


def gat(out, win, off, q="v"):
    if q == "v":
        op("v", lambda g, T: g.vector.tensor_copy(ap(T, out), ap(T, win).indirect(ap(T, off))), [win, off], [out], 0.05 + wid(out) * 1.56 * CY)
    else:
        op("s", lambda g, T: g.scalar.activation(ap(T, out), ap(T, win).indirect(ap(T, off)), AF.Copy), [win, off], [out], 0.065 + wid(out) * 1.56 * CY)


def gsub(out, win, off, b):
    gop(out, win, off, b, SUB)


def gop(out, win, off, b, o):
    op("v", lambda g, T: g.vector.tensor_tensor(ap(T, out), ap(T, win).indirect(ap(T, off)), ap(T, b), o), [win, off, b], [out], 0.05 + wid(out) * 1.56 * CY)


def scat(win, off, a):
    op("v", lambda g, T: g.vector.tensor_copy(ap(T, win).indirect(ap(T, off)), ap(T, a)), [a, off], [win], 0.05 + wid(a) * 3 * CY)


def tt(out, a, b, o):
    op("v", lambda g, T: g.vector.tensor_tensor(ap(T, out), ap(T, a), ap(T, b), o), [a, b], [out], max(64, wid(a) * (1 if is_ps(a) or is_ps(b) else 2)) * CY)


def ts(out, a, s1, s2, o0, o1=None):
    def fn(g, T):
        x1 = ap(T, s1) if isinstance(s1, tuple) else s1
        x2 = ap(T, s2) if isinstance(s2, tuple) else s2
        if o1 is None:
            return g.vector.tensor_scalar(ap(T, out), ap(T, a), x1, None, o0)
        return g.vector.tensor_scalar(ap(T, out), ap(T, a), x1, x2, o0, o1)
    op("v", fn, [a, _isr(s1), _isr(s2)], [out], max(64, wid(a) * (0.5 if two(out, a) else 1)) * CY)


def scan(out, d0, d1, init, o0, o1):
    op("v", lambda g, T: g.vector.tensor_tensor_scan(ap(T, out), ap(T, d0), ap(T, d1), init, o0, o1), [d0, d1], [out], max(64, wid(out)) * CY)


def fill(out, c):
    op("v", lambda g, T: g.vector.memset(ap(T, out), c), [], [out], max(64, wid(out) * (0.5 if two(out) else 1)) * CY)


def act(out, a, f=None, scale=1.0, bias=0.0, acc=None):
    def fn(g, T):
        kw = {}
        if isinstance(scale, tuple):
            kw["scale"] = ap(T, scale)
        elif scale != 1.0:
            kw["scale"] = scale
        if isinstance(bias, tuple):
            kw["bias"] = ap(T, bias)
        elif bias != 0.0:
            kw["bias"] = bias
        if acc:
            kw["accum_out"] = ap(T, acc)
        return g.scalar.activation(ap(T, out), ap(T, a), f or AF.Copy, **kw)
    op("s", fn, [a, _isr(scale), _isr(bias)], [out] + ([acc] if acc else []), 0.06 + wid(a) * CY)


def mm(group):
    mms([group])


def mms(groups):
    rd, wr, cost = [], [gr[0][0] for gr in groups], 0.0
    for gr in groups:
        for o, l, r in gr:
            for x in (l, r):
                if x not in rd:
                    rd.append(x)
            cost += max(min(64, wid(l)), wid(r)) * (1 if two(l) else 4) * 0.0006

    def fn(g, T):
        return [g.tensor.matmul(ap(T, o), ap(T, l), ap(T, r), k == 0, k == len(gr) - 1) for gr in groups for k, (o, l, r) in enumerate(gr)]
    op("t", fn, rd, wr, cost)


def iota(out, pat, base, cm):
    kw = {} if VS[out[0]][2] == "int32" else {"allow_small_or_imprecise_dtypes": True}
    op("g", lambda g, T: g.iota(ap(T, out), pat, base, cm, **kw), [], [out], 0.13 + 2 * wid(out) * CY)


def dma(q, sem, out, a, oap=None, aap=None, us=2.0):
    def fn(g, T):
        e = g.sync if q == "y" else g.scalar
        return e.dma_start(oap(T) if oap else ap(T, out), aap(T) if aap else ap(T, a))
    op(q, fn, [a], [out] if out else [], 0.1, us, "d_" + sem, 16)


def consts():
    iota(R("IT", 0, 1), [[0, 1]], 0, 1)
    iota(R("CI"), [[1, 192]], 0, 0)
    iota(R("C128"), [[1, 192]], 0, 0)
    iota(R("J"), [[0, 8], [1, SEG]], 0, 0)
    ts(R("IT", 1, 2), R("IT", 0, 1), 15, None, AluOpType.bitwise_and)
    ts(R("IT", 2, 3), R("IT", 0, 1), 4, None, AluOpType.arith_shift_right)
    cp(R("COL", 0, 3), R("IT", 0, 3))
    P, PLO, PHI = R("COL", 0, 1), R("COL", 1, 2), R("COL", 2, 3)
    tt(R("COL", 3, 4), P, PHI, ADD)
    ts(R("COL", 4, 5), PHI, 16.0, 15.0, MUL, ADD)
    ts(R("COL", 5, 6), P, 16.0, 15.0, MUL, ADD)
    for k in range(4):
        ts(R("COL", 6 + k, 7 + k), PLO, float(k), None, EQ)
    ts(R("COL", 10, 11), PLO, 1.5, None, LT)
    ts(R("CJ"), R("CI"), 15, None, AluOpType.bitwise_and)
    cp(R("CLO"), R("CJ"))
    ts(R("XI", 0, 144), R("CI", 0, 144), 4, None, AluOpType.arith_shift_right)
    cp(R("CHI"), R("XI", 0, 144))
    ts(R("ONEF"), R("CHI", 0, 128), PHI, None, EQ)
    ts(R("ONEB"), R("CHI", 0, 128), PHI, None, EQ)
    ts(R("BLK"), R("C128", 0, 8), PHI, 16.0, EQ, MUL)
    ts(R("BL"), R("C128", 0, 8), PHI, None, EQ)
    ts(R("T1", 0, 128), R("CLO", 0, 128), PLO, -1.0, LT, MUL)
    tt(R("TRIN"), R("T1", 0, 128), R("ONEF"), MUL)
    ts(R("ZW"), R("C128", 0, 144), R("COL", 4, 5), None, EQ)
    ts(R("Z8"), R("C128", 0, 144), R("COL", 5, 6), None, EQ)
    for k in range(3):
        ts(R("SEL%d" % k), R("ONEF"), R("COL", 6 + k, 7 + k), None, MUL)
    ts(R("MASK"), R("CLO"), PLO, None, EQ)
    ts(R("IDF"), R("C128", 0, 128), P, None, EQ)
    ts(R("IDB"), R("C128", 0, 128), P, None, EQ)
    ts(R("IDN"), R("C128", 0, 128), P, -1.0, EQ, MUL)
    ts(R("IT", 3, 4), R("IT", 2, 3), 1, None, AluOpType.bitwise_and)
    cp(R("COL", 11, 12), R("IT", 3, 4))
    ts(R("BLQ"), R("C128", 0, 8), R("COL", 11, 12), None, EQ)
    fill(R("O64"), 3264.0)
    ts(R("T2", 0, NSEG), R("C128", 0, NSEG), -1.0, None, ADD)
    ts(R("PERF"), R("T2", 0, NSEG), R("COL", 3, 4), None, EQ)
    ts(R("PERB"), R("PERF"), 262144.0, None, MUL)
    ts(R("RST"), R("J"), 0.0, 2e9, EQ, MUL)
    ts(R("RST"), R("RST"), -1e9, None, ADD)
    ts(R("CP1"), R("J"), 0.0, 3264.0, EQ, MUL)
    ts(R("T1", 0, NSEG), R("J"), -1.0, 0.0, ADD, MAX)
    ts(R("COL", 12, 13), PLO, 1.0, None, ADD)
    ts(R("RSM"), R("J"), 0.5, None, GT)
    ts(R("T2", 0, NSEG), R("J"), 4096.0, None, MUL)
    tt(R("CP2"), R("T2", 0, NSEG), R("CP1"), ADD)
    ts(R("T2", 0, NSEG), R("J"), 0.0, 131072.0, EQ, MUL)
    tt(R("CK"), R("T1", 0, NSEG), R("T2", 0, NSEG), ADD)
    fill(R("O1B"), 1.0)
    fill(R("O1F"), 1.0)
    ts(R("LW", 0, 6), R("C128", 0, 6), 16.0, PLO, MUL, ADD)
    ts(R("KB", 0, 6), R("LW", 0, 6), 0.5, None, ADD)
    ts(R("KROW"), R("C128", 0, 96), 4097.0, None, ADD)
    for k in range(3):
        ts(R("DUM", 6 * k, 6 * k + 6), R("LW", 0, 6), float(W + (96 if k == 1 else 0)), None, ADD)
    ts(R("DS1", 0, 6), R("LW", 0, 6), 33.0, None, ADD)
    ts(R("DUMR"), R("C128", 0, 32), float(W + 192), None, ADD)
    ts(R("DUMW", 0, 2), R("LW", 0, 2), float(W + 192), None, ADD)
    ts(R("RS16"), R("CLO"), 0.5, None, GT)
    ts(R("TRIB"), R("CLO", 0, 16), PLO, 20000.0, LE, MUL)
    ts(R("T2", 0, 128), R("IDF"), 4096.0, None, MUL)
    tt(R("TRI2"), R("T2", 0, 128), R("TRIN"), ADD)
    ts(R("ONEL"), R("ONEF"), PLO, None, MUL)
    ts(R("COL", 13, 14), R("COL", 6, 7), -1.0, None, MUL)
    ts(R("COL", 14, 15), R("COL", 7, 8), -1.0, 1.0, MUL, ADD)
    for t in range(1, 4):
        ts(R("NC", 32 * t - 32, 32 * t), R("C128", 0, 32), float(16 + 32 * (t - 1)), R("COL", 6 + t, 7 + t), ADD, MUL)
    for t in range(4):
        s = 66 * t
        iota(R("VAL%d" % t, 0, NB - s), [[16, NB - s]], 16 * s, 0)
        if s:
            iota(R("VAL%d" % t, NB - s, NB), [[16, s]], 0, 0)
        iota(R("VAL%d" % t, NB, 216), [[0, 216 - NB]], M, 0)
    fill(R("P2", 0, 2 * NSEG), 0.0)
    fill(R("RK", NB, 212), 0.0)
    fill(R("OKR", NB, 212), 0.0)
    fill(R("NGB", 204, 212), 0.0)
    for t in range(3):
        fill(R("MB%d" % t), 0.0)
        fill(R("FNW%d" % t), 0.0)


def load():
    dma("y", "gin", R("GD"), None, aap=lambda T: T.gn[:, :], us=2.5)
    dma("a", "fin", R("FD"), None, aap=lambda T: T.fa[:, :], us=2.5)
    c = M // 4
    for k in range(4):
        dma("y", "sn%d" % k, R("SNW", c * k, c * k + c), None, aap=lambda T, k=k: T.sn[:, c * k:c * k + c], us=3.0 + 1.5 * k)
    dma("a", "win", R("WC"), None, aap=lambda T: T.w[:, :], us=2.0)
    dma("a", "xin", R("XW", 0, M), None, aap=lambda T: T.x[:, :], us=9.0)
    iota(R("FGW"), [[0, FGWW]], 0, 0)
    ts(R("GDB"), R("GD"), 3.0, None, LT)
    cp(R("GDF"), R("GD"))
    cp(R("FDF"), R("FD"))
    wh = lambda n: (n, 0, M, 1, 0, 8, 1)
    dma("a", "gb1", wh("DGB"), R("GDB"))
    dma("a", "ff1", wh("DFF"), R("FDF"))
    dma("a", "gf1", wh("DGF"), R("GDF"))
    dma("a", "gb2", R("GB8", p1=8), wh("DGB"))
    fill(R("F1R", M, FGWW), 0.0)
    fill(R("F2R", M, FGWW), 0.0)
    for k in (1, 2):
        op("y", lambda g, T, k=k: [g.sync.dma_start(T["F%dR" % k][i:128:16, 0:M], T.DFF[:, :]) for i in range(16)], [wh("DFF")], [R("F%dR" % k, 0, M)], 1.6, 5.0, "d_ff%d" % (k + 1), 16)
    dma("a", "gf2", R("FGW", 0, M, p0=2, ps=16), wh("DGF"))
    fill(R("SNW", M, SNWW), 3264)
    fill(R("XW", M, M + 16), BIGX)
    fill(R("XW", M + 16, XWW), 0.0)
    fill(R("BAD", M, BADW), 1.0)


def load2():
    c = M // 4
    for k in range(4):
        ts(R("BAD", c * k, c * k + c), R("SNW", c * k, c * k + c), 3264.0, None, NEQ)
    mm([(R("P3", 0, 204), R("Z8", 15 - lo, 143 - lo, p1=8), R("GB8", lo, M, 16, p1=8)) for lo in range(16)])
    ts(R("NGB", 0, 204), R("P3", 0, 204), -1.0, None, MUL)
    ts(R("WB"), R("ONEB"), R("WC"), None, MUL)


def diag(src, n, k, msk=True):
    m, s = R("DGM", 192 * k, 192 * k + n), R("DGS", 192 * k, 192 * k + n)
    tt(m, src, R("MASK", 0, n), MUL)
    scan(s, R("RS16", 0, n), m, 0.0, MUL, ADD)
    return R("DGS", 192 * k + 15, 192 * k + n, 16)


def level(ch, bank, nl, off, bar, xle, last):
    CLS[0] = ch
    kc = nl // 16
    sf, su, dd = R("SF" + ch), R("SU" + ch), "DD" + ch
    gat(su, R("SNW", 0, W), off)
    cp(sf, su)
    cpr = R("CP2" if last else "CP1", p1=1)
    pt, pk, pw = R(bank, 0, NSEG, p1=nl), R(bank, NSEG, 2 * NSEG, p1=nl), R(bank, 300, 300 + kc)
    mm([(pt, R("O1B", 0, nl, p1=1), cpr), (pt, sf, R("PERF"))])
    keys = [(pk, R("O1B", 0, nl, p1=1), R("CK", p1=1))]
    if bar:
        tt(R("EQ" + ch), sf, bar, EQ)
        keys.append((pk, R("EQ" + ch), R("PERB")))
    differences(ch, dd, xle)
    for s in range(16):
        keys.append((R(bank, NSEG + 1 + s, 2 * NSEG, SEG, p1=nl), R(dd, s, 16 * nl, 16), R("BLK")))
    mm(keys)
    argmin(ch, pk, pt, nl, 8, last)
    mm([(pw, R("AA" + ch, p1=nl), R("BL", 0, kc, p1=nl))])
    return pw


def differences(ch, dd, xle):
    at = 0
    for e, n in CH[ch]:
        a, b = 16 * at, 16 * (at + n)
        if e == "v":
            gsub(R(dd, a, b), R("XW", 0, W), R("SU" + ch, at, at + n), R(xle, a, b))
            act(R(dd, a, b), R(dd, a, b), AF.Abs)
        else:
            gat(R(dd, a, b), R("XW", 0, W), R("SU" + ch, at, at + n), "s")
            ps = R("P7" if ch == "R" else "P5", 0, b - a)
            mm([(ps, R("IDB"), R(dd, a, b)), (ps, R("IDN"), R(xle, a, b))])
            act(R(dd, a, b), ps, AF.Abs)
        at += n


def argmin(ch, pk, pt, np_, ns, last=False):
    k = SEG * ns
    wk = [R("WK" + ch, NSEG * j, NSEG * j + k, p1=np_) for j in range(5)]
    scan(wk[0], R("RST", 0, k, p1=np_), pk, 0.0, MAX, MIN)
    tt(wk[1], pk, wk[0], EQ)
    if last:
        tt(wk[3], wk[1], pt, MUL)
        scan(wk[4], R("RSM", 0, k, p1=np_), wk[3], 0.0, MUL, MAX)
    else:
        if NR[ch] == "s":
            act(wk[2], wk[1], AF.Copy, scale=-1.0, bias=1.0)
        else:
            ts(wk[2], wk[1], -1.0, 1.0, MUL, ADD)
        tt(wk[3], wk[1], pt, MUL)
        scan(wk[4], wk[2], wk[3], 0.0, MUL, ADD)
    for gi in range(ns):
        o, z = R("AA" + ch, 16 * gi, 16 * gi + 16, p1=np_), 4 * NSEG + SEG * gi + 16
        if gi < ns - AV[ch]:
            act(o, R("MASK", 0, 16, p1=np_), AF.Copy, scale=R("WK" + ch, z, z + 1, p1=np_))
        else:
            ts(o, R("MASK", 0, 16, p1=np_), R("WK" + ch, z, z + 1, p1=np_), None, MUL)


def guest_level(off):
    sf, su, dd = R("SFR"), R("SUR"), "DDR"
    gat(su, R("SNW", 0, W), off)
    cp(sf, su)
    differences("R", dd, "XLR")
    n = GQ[0]
    qs = [(q, {"p0": 16 * n * q, "p1": 16 * n * q + 32}) for q in range(8 // n)]
    k = n * SEG
    mms([[(R("P2", 0, k, **p), R("O1B", 0, 32, p1=1), R("CP1", 0, k, p1=1)), (R("P2", 0, k, **p), sf, R("PERF", k * q, k * q + k))] for q, p in qs])
    mms([[(R("P2", k, 2 * k, **p), R("O1B", 0, 32, p1=1), R("CK", 0, k, p1=1))]
         + [(R("P2", k + 1 + s, 2 * k, SEG, **p), R(dd, s, 512, 16), R("BLK", n * q, n * q + n)) for s in range(16)] for q, p in qs])
    argmin("R", R("P2", k, 2 * k), R("P2", 0, k), 128, n)
    mms([[(R("P2", 300, 302, p0=p["p0"], p1=p["p0"] + 16 * n), R("AAR", 0, 16 * n, **p), R("BLQ", 0, 2, **p))] for q, p in qs])
    return R("P2", 300, 302)


def arrivals(t):
    ar = "AR%d" % t
    op("n", None, [R("MB%d" % (t - 1), 0, 64)], [R(ar)], 0.0, 3.0, "ar%d" % t, NENG)
    for k in range(16):
        act(R("XLR", k, 512, 16), R(ar, 32, 64))
    mm([(R("P2", 310, 342), R("WB"), R(ar, 32, 64))])
    mm([(R("P2", 342, 374), R("SEL2"), R(ar, 0, 32))])
    cp(R("RI"), R("P2", 310, 342))
    ts(R("RI2"), R("RI"), 63, None, AluOpType.bitwise_and)
    tt(R("DGM", 384, 416), R("RI2"), R("MASK", 0, 32), MUL)
    tt(R("DGM", 416, 448), R("P2", 342, 374), R("MASK", 0, 32), MUL)
    scan(R("DGS", 384, 448), R("RS16", 0, 64), R("DGM", 384, 448), 0.0, MUL, ADD)
    cp(R("LU", 32, 34), R("DGS", 384 + 15, 416, 16))
    cp(R("RW", 0, 2), R("DGS", 416 + 15, 448, 16))
    for k in (3, 4, 5):
        ts(R("RW", 2 * k, 2 * k + 2), R("RW", 0, 2), float(k + 1), None, EQ)
    for k in range(1, 6):
        pw = guest_level(R("LU", 32 + 2 * k - 2, 32 + 2 * k))
        if k < 5:
            cp(R("LU", 32 + 2 * k, 34 + 2 * k), pw)
        if k >= 3:
            ts(R("RW", 12, 14), pw, -3264.0, None, ADD)
            tt(R("RW", 14 + 2 * k, 16 + 2 * k), R("RW", 12, 14), R("RW", 2 * k, 2 * k + 2), MUL)
            if k == 4:
                tt(R("RW", 26, 28), R("RW", 20, 22), R("RW", 22, 24), ADD)
    tt(R("RW", 28, 30), R("RW", 26, 28), R("RW", 24, 26), ADD)
    ts(R("LU", 42, 44), R("RW", 28, 30), 3264.0, None, ADD)
    gat(R("RB%d" % t), R("XW", 0, W), R("LU", 42, 44))
    op("g", ("ret", t), [R("RB%d" % t)], [], 0.6, 1.0, "ls", NENG)


def lanes(t):
    mm([(R("P3", 0, NB), R("ZW", 15 - lo, 143 - lo), R("BAD", lo, W, 16)) for lo in range(16)])
    s = 66 * t
    tt(R("OKR", 0, NB - s), R("P3", s, NB), R("NGB", s, NB), EQ)
    if s:
        tt(R("OKR", NB - s, NB), R("P3", 0, s), R("NGB", 0, s), EQ)
    tot, pre = R("P3", 256, 256 + NB), R("P3", 0, NB)
    mm([(tot, R("ONEB"), R("OKR", 0, NB))])
    mm([(pre, R("TRI2"), R("OKR", 0, NB))])
    scan(R("CUM"), R("O1F", 0, NB), tot, 0.0, MUL, ADD)
    for k in range(6):
        act(R("SJ", NB * k, NB * k + NB), R("CUM"), AF.Sign, scale=-1.0, bias=R("KB", k, k + 1), acc=R("HR", k, k + 1))
    tt(R("RK", 0, NB), R("CUM"), pre, ADD)
    ts(R("RHO", 0, 6), R("HR", 0, 6), 0.5, NB / 2, MUL, ADD)
    gat(R("VG"), R("VAL%d" % t, 0, 212), R("RHO", 0, 6), "s")
    gop(R("OH"), R("RK"), R("RHO", 0, 6), R("KROW"), EQ)
    mm([(R("P4", 0, 96), R("IDB"), R("VG")), (R("P4", 0, 96), R("ONEL"), R("OH"))])
    hs = diag(R("P4", 0, 96), 96, 0)
    cp(R("LU", 0, 6), hs)
    act(R("HREP"), R("P4", 0, 96))
    act(R("HW", 0, 6), hs)
    ft = "F%dR" % (1 + t % 2)
    gop(R("DGM", 192, 288), R(ft, 0, W), R("LU", 0, 6), R("MASK", 0, 96), MUL)
    scan(R("DGS", 192, 288), R("RS16", 0, 96), R("DGM", 192, 288), 0.0, MUL, ADD)
    ps = R("DGS", 192 + 15, 288, 16)
    cp(R("LU", 6, 12), ps)
    act(R("PWF", 0, 6), ps)
    gat(R("PREP"), R(ft, 0, W), R("LU", 0, 6), "s")
    gop(R("DGM", 0, 96), R(ft, 0, W), R("LU", 6, 12), R("MASK", 0, 96), MUL)
    scan(R("DGS", 0, 96), R("RS16", 0, 96), R("DGM", 0, 96), 0.0, MUL, ADD)
    cp(R("LU", 12, 18), R("DGS", 15, 96, 16))
    gat(R("FH"), R("FGW", 0, W), R("LU", 0, 6), "s")
    gat(R("XL"), R("XW", 0, W), R("LU", 0, 6))
    for k in range(16):
        if k % 2:
            act(R("XLE", k, 1536, 16), R("XL"))
        else:
            cp(R("XLE", k, 1536, 16), R("XL"))


def w6(k, n=6):
    return R("W6", 6 * k, 6 * k + n)


def own(t):
    pa = level("A", "P0", 96, R("LU", 6, 12), R("P4", 0, 96), "XLE", False)
    cp(R("LU", 18, 24), pa)
    act(w6(1), pa)
    pb = level("B", "P1", 96, R("LU", 12, 18), R("PREP"), "XLE", False)
    cp(R("LU", 24, 30), pb)
    pa = level("A", "P0", 96, R("LU", 18, 24), None, "XLE", True)
    act(w6(0), pa)
    pb = level("B", "P1", 96, R("LU", 24, 30), None, "XLE", False)
    cp(R("LU", 46, 52), pb)
    act(w6(3), pb)
    pb = level("B", "P1", 96, R("LU", 46, 52), None, "XLE", True)
    CLS[0] = "T"
    ts(w6(7), R("HW", 0, 6), 3264.0, None, NEQ)
    ts(w6(9), R("PWF", 0, 6), 64.0, None, GE)
    tt(w6(9), w6(9), w6(7), MUL)
    ts(w6(4), w6(0), 3264.0, None, NEQ)
    ts(w6(5), w6(0), 3264.0, None, EQ)
    tt(w6(11), w6(4), w6(7), MUL)
    tt(w6(23), w6(9), w6(5), MUL)
    tt(w6(24), w6(4), w6(0), MUL)
    tt(w6(25), w6(4), w6(1), MUL)
    tt(w6(8), w6(5), w6(3), MUL)
    tt(w6(8), w6(8), w6(25), ADD)
    ts(w6(26), w6(8), 5.0, None, ADD)
    ts(w6(6), pb, 3264.0, None, NEQ)
    tt(w6(6), w6(6), w6(23), MUL)
    tt(w6(10), w6(6), w6(11), ADD)
    tt(w6(28), pb, w6(5), MUL)
    tt(R("I6", 0, 6), w6(28), w6(24), ADD)
    ts(R("I6", 6, 12), R("I6", 0, 6), 4095, None, AluOpType.bitwise_and)
    ts(R("I6", 12, 18), R("I6", 0, 6), 12, None, AluOpType.arith_shift_right)
    cp(R("LU", 52, 58), R("I6", 6, 12))
    cp(R("LU", 58, 64), w6(8))
    if t < 3:
        CLS[0] = "S"
        send(t)
        CLS[0] = "T"
    cp(w6(12, 12), R("I6", 6, 18))
    ts(w6(27), R("I6", 6, 12), 5.0, None, ADD)
    tt(w6(15), w6(26), w6(10), MUL)
    tt(w6(16), w6(27), w6(10), MUL)
    for b, k, q in (("EXY", 26, 1), ("EXS", 27, 1), ("EXA", 13, 1)):
        for l in range(6):
            o, sc = R(b, 16 * l, 16 * l + 16), R("W6", 6 * k + l, 6 * k + l + 1)
            if q:
                act(o, R("MASK", 0, 16), AF.Copy, scale=sc)
            else:
                ts(o, R("MASK", 0, 16), sc, None, MUL)
    sr, ar, cfl = R("P4", 96, 192), R("P4", 288, 384), R("P4", 384, 480)
    cf = []
    for v, b, bank in ((0, "EXY", "P6"), (1, "EXS", "P3")):
        at, gr = 0, []
        for l in range(6):
            n = 96 - 16 * l
            gr.append([(R(bank, at, at + n), R("ONEF"), R(b, 16 * l, 96)), (R(bank, at, at + 16), R("IDB"), R("TRIB"))])
            at += n
        mms(gr)
        at = 0
        for l in range(6):
            n = 96 - 16 * l
            ts(R("EQP", 336 * v + at, 336 * v + at + n), R(bank, at, at + n), R("W6", 6 * (15 + v) + l, 6 * (15 + v) + l + 1), None, EQ)
            cf.append((R("P4", 384 + 16 * l, 480), R("ONEB"), R("EQP", 336 * v + at, 336 * v + at + n)))
            at += n
    mm([(sr, R("ONEF"), R("EXS"))])
    mm([(ar, R("ONEB"), R("EXA"))])
    mm(cf)
    gat(R("SY"), R("SNW", 0, W), R("LU", 58, 64))
    ts(R("NEY"), R("SY"), 3264.0, None, NEQ)
    sv = R("P4", 192, 288)
    mm([(sv, R("ONEB"), R("NEY"))])
    ts(R("SEV"), sv, 1.5, None, GT)
    for l in range(6):
        act(R("FR", 16 * l, 16 * l + 16), R("MASK", 0, 16), AF.Copy, scale=R("W6", 60 + l, 61 + l))
    tt(R("ADB", 0, 96), cfl, R("FR"), LT)
    tt(R("ADB", 96, 192), R("ADB", 0, 96), R("SEV"), MUL)
    scan(R("DGS", 0, 192), R("RS16"), R("ADB"), 0.0, MUL, ADD)
    ad = R("DGS", 15, 192, 16)
    tt(w6(17), R("HW", 0, 6), R("DUM", 0, 6), SUB)
    tt(w6(18), w6(8), R("DUM", 6, 12), SUB)
    tt(w6(19), w6(12), R("DUM", 12, 18), SUB)
    tt(w6(20, 12), w6(17, 12), ad, MUL)
    tt(w6(22), w6(19), R("DGS", 15, 96, 16), MUL)
    tt(w6(20, 18), w6(20, 18), R("DUM"), ADD)
    hl, hyl, sl = R("LU3", 0, 6), R("LU3", 0, 12), R("LU3", 12, 18)
    cp(R("LU3", 0, 18), w6(20, 18))
    gat(R("XS"), R("XW", 0, W), R("LU", 52, 58), "s")
    px = R("P6", 336, 432)
    mm([(px, R("IDB"), R("XS")), (px, R("IDB"), R("XL"))])
    ts(R("XI", 96, 192), px, 0.5, -0.25, MUL, ADD)
    tt(w6(30), w6(19), R("DGS", 96 + 15, 192, 16), MUL)
    tt(w6(30), w6(30), R("DUM", 12, 18), ADD)
    cp(R("LU3", 18, 24), w6(30))
    if t < 3:
        ts(R("NHF"), sr, -3269.0, R("COL", 6, 7), ADD, MUL)
        ts(R("NHY", 0, 96), R("NHF"), 3264.0, None, ADD)
        ts(R("SLM"), ar, R("COL", 12, 13), None, EQ)
        ts(R("GY"), R("SY"), -1.0, 3264.0, MUL, ADD)
        tt(R("GY"), R("GY"), R("SLM"), MUL)
        tt(R("NHY", 96, 192), R("GY"), R("SY"), ADD)
        scat(R("BAD"), hl, R("O1B", 0, 96))
        scat(R("SNW"), hyl, R("NHY"))
    scat(R("F2R"), sl, R("HREP"))
    scat(R("F1R"), R("LU3", 18, 24), R("HREP"))
    scat(R("XW"), sl, R("XI", 96, 192))


_d("LU3", 24, "uint16")


def send(t):
    fn, mb = "FNW%d" % t, "MB%d" % t
    tt(R("LS6", 0, 6), w6(7), w6(10), SUB)
    tot, pre = R("P4", 480, 486), R("P4", 488, 494)
    mm([(tot, R("ONEB"), R("LS6", 0, 6))])
    mm([(pre, R("TRIN"), R("LS6", 0, 6))])
    scan(R("RW2", 0, 6), R("O1F", 0, 6), tot, 0.0, MUL, ADD)
    tt(R("RW2", 6, 12), R("RW2", 0, 6), pre, ADD)
    ts(R("RW2", 12, 18), R("RW2", 6, 12), 32.5, None, LT)
    tt(R("RW2", 12, 18), R("RW2", 12, 18), R("LS6", 0, 6), MUL)
    tt(R("RW2", 18, 24), R("RW2", 6, 12), R("DS1", 0, 6), SUB)
    tt(R("RW2", 18, 24), R("RW2", 18, 24), R("RW2", 12, 18), MUL)
    tt(R("RW2", 18, 24), R("RW2", 18, 24), R("DS1", 0, 6), ADD)
    ts(R("LUS", 0, 6), R("RW2", 18, 24), -1.0, None, ADD)
    ts(R("FN1"), R("FH"), 1.0, R("COL", 8, 9), ADD, MUL)
    act(R("FN2"), R("HREP"), AF.Copy, scale=R("COL", 10, 11))
    tt(R("FN1"), R("FN1"), R("FN2"), ADD)
    scat(R(fn), R("LUS", 0, 6), R("FN1"))
    scat(R(mb, 32, 160), R("LUS", 0, 6), R("XL"))
    ts(R(mb, 0, 32), R(fn, 0, 32), R("COL", 8, 9), None, MUL)
    op("g", ("send", t), [R(mb, 0, 64)], [], 0.6, 1.0, "ls", NENG)


_d("RW2", 24)
_d("LUS", 8, "uint16")


def comeback(t):
    rr, fn = "RR%d" % t, "FNW%d" % (t - 1)
    op("n", None, [R("RB%d" % t)], [R(rr)], 0.0, 3.0, "rr%d" % t, NENG)
    a = 3280 + 32 * (t - 1)
    mm([(R("P2", 374, 406), R("SEL0"), R(fn, 0, 32))])
    act(R("HPR"), R("P2", 374, 406))
    if t < 3:
        tt(R("HPD"), R("P2", 374, 406), R("DUMR"), SUB)
        tt(R("HPD"), R("HPD"), R("MASK", 0, 32), MUL)
    ts(R("FL"), R(rr), 1000.0, None, LT)
    if t < 3:
        tt(R("FLN"), R("FL"), R("HPD"), MUL)
        scan(R("DGS", 448, 480), R("RS16", 0, 32), R("FLN"), 0.0, MUL, ADD)
        tt(R("RW", 30, 32), R("DGS", 448 + 15, 480, 16), R("DUMW", 0, 2), ADD)
        cp(R("LU", 44, 46), R("RW", 30, 32))
        scat(R("BAD"), R("LU", 44, 46), R("O1B", 0, 32))
        ts(R("BAD", a, a + 32), R(rr), 1000.0, None, GE)
        gat(R("CUR"), R("SNW"), R("LU", 44, 46))
        tt(R("FLN"), R("FL"), R("NC", 32 * t - 32, 32 * t), MUL)
        tt(R("CUR2"), R("CUR"), R("FLN"), ADD)
        scat(R("SNW"), R("LU", 44, 46), R("CUR2"))
    tt(R("XW", a, a + 32), R(rr), R("FL"), MUL)
    tt(R("F1R", a, a + 32), R("HPR"), R("FL"), MUL)
    tt(R("F2R", a, a + 32), R("HPR"), R("FL"), MUL)
    if t < 3:
        tt(R("FGW", a, a + 32), R(fn, 0, 32), R("FL"), MUL)


def store():
    fill(R("XW", M, M + 16), 0.0)
    dma("y", "o1", None, R("XW", 0, W), oap=lambda T: T.xo[:, :], us=6.0)
    dma("a", "o2", None, R("F1R", 0, W, p0=0, ps=16), oap=lambda T: T.fo[:, :], us=4.0)
    dma("y", "o3", None, R("F2R", 0, W, p0=0, ps=16), oap=lambda T: T.f2o[:, :], us=4.0)


def schedule():
    load()
    consts()
    load2()
    for t in range(NT):
        if t:
            CLS[0] = "R"
            arrivals(t)
        CLS[0] = "L"
        lanes(t)
        own(t)
        if t:
            CLS[0] = "C"
            comeback(t)
    CLS[0] = "I"
    store()
    last = {}
    for o in OPS:
        dep = set()
        qq = "s" if o["q"] == "a" else o["q"]
        for kind, lst in (("r", o["rd"]), ("w", o["wr"])):
            for r in lst:
                ps = is_ps(r)
                for (k2, r2, j) in last.get(r[0], []):
                    if ps:
                        if OPS[j]["q"] != o["q"] or ((kind == "w" or k2 == "w") and hit(r, r2)):
                            dep.add(j)
                    elif (kind == "w" or k2 == "w") and hit(r, r2):
                        dep.add(j)
        o["dep"] = sorted(dep)
        for kind, lst in (("r", o["rd"]), ("w", o["wr"])):
            for r in lst:
                h = last.setdefault(r[0], [])
                if kind == "w" and not is_ps(r):
                    h[:] = [e for e in h if not (r[3] == 1 and r[6] == 1 and e[1][1] >= r[1] and e[1][2] <= r[2] and e[1][4] >= r[4] and e[1][5] <= r[5])]
                h.append((kind, r, o["i"]))
    n = len(OPS)
    succ = [[] for _ in range(n)]
    for o in OPS:
        for j in o["dep"]:
            succ[j].append(o["i"])
    rank = [0.0] * n
    for i in range(n - 1, -1, -1):
        o = OPS[i]
        rank[i] = o["cost"] + o["tail"] + max([rank[j] + WAKE for j in succ[i]], default=0.0)
    rank = [r + BON[o["c"]] for r, o in zip(rank, OPS)]
    left = [len(o["dep"]) for o in OPS]
    ready = {i: 0.0 for i in range(n) if not left[i]}
    free, end, order = {}, [0.0] * n, []
    while ready:
        best = None
        for i, rt in ready.items():
            q = "s" if OPS[i]["q"] == "a" else OPS[i]["q"]
            st = max(rt, free.get(q, 0.0)) if q != "n" else rt
            key = (st, -rank[i], i)
            if best is None or key < best[0]:
                best = (key, i, q, st)
        _, i, q, st = best
        if q != "n" and OPT["slack"]:
            lim, top = st + OPT["slack"], rank[i]
            for j, rt in ready.items():
                if ("s" if OPS[j]["q"] == "a" else OPS[j]["q"]) == q and rank[j] > top + OPT["slack"] and max(rt, free.get(q, 0.0)) <= lim:
                    i, top, st = j, rank[j], max(rt, free.get(q, 0.0))
        del ready[i]
        o = OPS[i]
        if q != "n":
            free[q] = st + o["cost"]
        end[i] = st + o["cost"] + o["tail"]
        order.append(i)
        for j in succ[i]:
            left[j] -= 1
            if not left[j]:
                ready[j] = max(end[d] + (WAKE if OPS[d]["q"] != "n" else 0.0) for d in OPS[j]["dep"])
    return order, max(end)


PLAN = {}
QSEM = {"v": "sv", "s": "ss", "t": "st", "g": "sg"}


def rank_program(g, core, T, topo):
    rank = T.rank_of(core)
    if rank is None:
        return
    if not PLAN:
        PLAN["order"], PLAN["est"] = schedule()
    eng = {"v": g.vector, "s": g.scalar, "a": g.scalar, "t": g.tensor, "g": g, "y": g.sync}
    done, total, seen = {}, {}, {q: {} for q in "vstgy"}

    def remote(dst, out, src, sem):
        rid, pid, _ = topo.addr(dst)
        m = 0
        for e in topo.engines(core, dst)[:NENG]:
            m |= 1 << e
        g.remote_dma(out_ap=out, in_ap=src, remote_sem=T.sem[sem], local_sem=T.sem.ls, pid=pid, routing_id=rid, dma_engine_mask=m)

    for i in PLAN["order"]:
        o = OPS[i]
        if o["q"] == "n":
            total[o["sem"]] = o["n"]
            done[i] = (o["sem"], o["n"])
            continue
        q = "s" if o["q"] == "a" else o["q"]
        need = {}
        for j in o["dep"]:
            if OPS[j]["sem"] == "ls":
                continue
            s, v = done[j]
            need[s] = max(need.get(s, 0), v)
        for s in sorted(need):
            if seen[q].get(s, 0) < need[s]:
                eng[o["q"]].wait_ge(T.sem[s], need[s])
                seen[q][s] = need[s]
        fn = o["fn"]
        if isinstance(fn, tuple):
            what, t = fn
            if what == "send":
                remote(T.cores[(rank + 1 + t) % 8], T["AR%d" % (t + 1)][:, :], T["MB%d" % t][:, 0:64], "ar%d" % (t + 1))
            else:
                remote(T.cores[(rank - t) % 8], T["RR%d" % t][:, :], T["RB%d" % t][:, :], "rr%d" % t)
            total["ls"] = total.get("ls", 0) + NENG
            done[i] = ("ls", total["ls"])
            continue
        r = fn(g, T)
        s = o["sem"] or QSEM[o["q"]]
        for x in (r if isinstance(r, list) else [r]):
            x.then_inc(T.sem[s], o["n"])
            total[s] = total.get(s, 0) + o["n"]
        done[i] = (s, total[s])
    for s in sorted(total):
        if seen["g"].get(s, 0) < total[s]:
            g.wait_ge(T.sem[s], total[s])
